import numpy as np
import ml_dtypes


def mxq(x, axis, fmt="e4m3"):
    dtype, down = {"e4m3": (ml_dtypes.float8_e4m3fn, 7), "e5m2": (ml_dtypes.float8_e5m2, 14)}[fmt]
    v = np.moveaxis(np.asarray(x, np.float32).astype(ml_dtypes.bfloat16).astype(np.float64), axis, -1)
    blocks = v.reshape(v.shape[:-1] + (-1, 32))
    amax = np.abs(blocks).max(-1, keepdims=True)
    byte = np.maximum(np.where(amax > 0, np.frexp(amax)[1] - 1 + 127, 0) - down, 1)
    scale = np.exp2(byte - 127.0)
    codes = (blocks / scale).astype(np.float32).astype(dtype).astype(np.float64)
    return np.moveaxis((codes * scale).reshape(v.shape), -1, axis)


WIDE = False


def mx_kscale(k):
    if not WIDE:
        return np.ones(k)
    levels = np.array([10, -10, 5, -5, 0])
    if k % 512:
        return np.exp2(np.random.permutation(np.resize(levels, k // 32))).repeat(32)
    a = np.empty((k // 512, 16))
    for p in range(k // 512):
        a[p, :8] = np.random.permutation(np.resize(levels, 8))
        for g in range(8):
            far = levels[np.abs(levels - a[p, g]) >= 10]
            a[p, g + 8] = far[np.random.randint(len(far))]
    return np.exp2(a.ravel()).repeat(32)


def f64(x):
    return np.asarray(x).astype(np.float64)


def striped8(idx):
    return np.concatenate([v.reshape(-1, 16).T for v in idx]).astype(np.uint16)


def unstriped8(offs):
    return np.stack([offs[16 * g:16 * g + 16].T.reshape(-1) for g in range(8)]).astype(np.int64)


E2M1 = np.array([0.0, 0.5, 1.0, 1.5, 2.0, 3.0, 4.0, 6.0, -0.0, -0.5, -1.0, -1.5, -2.0, -3.0, -4.0, -6.0])


def pack_weight(w, fmt):
    k, n = w.shape
    w = f64(np.asarray(w, np.float32).astype(ml_dtypes.bfloat16)).reshape(k // 32, 32, n)
    amax = np.abs(w).max(1)
    if fmt == "e4m3":
        byte = np.frexp(amax)[1] - 1 + 127 - 7
    else:
        mant, ex = np.frexp(amax / 6.0)
        byte = np.where(mant > 0.5, ex, ex - 1) + 127
    byte = np.clip(np.where(amax > 0, byte, 1), 1, 254)
    scaled = (w * np.exp2(127.0 - byte)[:, None, :]).reshape(k, n).astype(np.float32)
    by_word = np.ascontiguousarray(scaled.reshape(k // 512, 128, 4, n).transpose(0, 1, 3, 2))
    if fmt == "e4m3":
        words = by_word.astype(ml_dtypes.float8_e4m3fn).view(np.uint8)
    else:
        c = by_word.astype(ml_dtypes.float4_e2m1fn).view(np.uint8) & 0xF
        words = (c[..., 0::2] | (c[..., 1::2] << 4)).reshape(k // 512, 128, 2 * n)
    return np.ascontiguousarray(words), np.ascontiguousarray(byte.astype(np.uint8).reshape(k // 512, 16, n))


def unpack_weight(words, scales, fmt):
    g, _, n = scales.shape
    words = np.ascontiguousarray(words).reshape(g, 128, n, -1)
    if fmt == "e4m3":
        vals = words.view(ml_dtypes.float8_e4m3fn).astype(np.float64)
    else:
        nib = np.empty((g, 128, n, 4), np.uint8)
        nib[..., 0::2] = words & 0xF
        nib[..., 1::2] = words >> 4
        vals = E2M1[nib]
    vals = vals * np.repeat(np.exp2(scales.astype(np.float64) - 127.0), 8, axis=1)[..., None]
    return vals.transpose(0, 1, 3, 2).reshape(g * 512, n)


K, M, T, S = 512, 1024, 1024, 512


def setup_inputs():
    n = np.random.standard_normal
    s = mx_kscale(K)[:, None]
    p_w = pack_weight(n((K, M)) / np.sqrt(K) / s, "e4m3")
    return {
        "xT": (n((K, T)) * s).astype(np.float32),
        "w_words": p_w[0],
        "w_scales": p_w[1],
        "wgt": np.repeat(np.random.uniform(0.5, 2.0, (8, S)), 16, axis=0).astype(np.float32),
        "b": (0.3 * n(1024)).astype(np.float32),
        "wgo": np.repeat(np.random.uniform(0.5, 2.0, (8, S)), 16, axis=0).astype(np.float32),
        "offs": striped8(np.stack([np.random.permutation(T)[:S] for _ in range(8)])),
        "offs2": striped8(np.stack([np.random.permutation(T)[:S] for _ in range(8)])),
    }


def reference(xT, w_words, w_scales, wgt, b, wgo, offs, offs2):
    idx = unstriped8(offs)
    group = np.arange(K) % 512 // 64
    xg = f64(wgt)[np.arange(K) // 4 % 128] * f64(xT)[np.arange(K)[:, None], idx[group]]
    xT_ = mxq(xg, 0, "e4m3")
    w_ = unpack_weight(w_words, w_scales, "e4m3")
    y = w_.T @ xT_
    place = unstriped8(offs2)[np.arange(M) % 128 // 16]
    out = np.zeros((M, T))
    out[np.arange(M)[:, None], place] = f64(wgo)[np.arange(M) % 128] * (y + f64(b)[:, None])
    return out

@@ -1,0 +1,154 @@
+import concourse.mybir as mybir
+from concourse.masks import make_identity
+
+K, M, T, S = 512, 1024, 1024, 512
+FLOPS = 2 * K * M * S
+
+F32 = mybir.dt.float32
+BF16 = mybir.dt.bfloat16
+I32 = mybir.dt.int32
+U32 = mybir.dt.uint32
+U16 = mybir.dt.uint16
+U8 = mybir.dt.uint8
+FP8X4 = mybir.dt.float8_e4m3fn_x4
+MULT = mybir.AluOpType.mult
+IDENTITY = mybir.ActivationFunctionType.Identity
+
+P = 128
+PLANES = 4
+HALF = S // 2
+N_TILES = M // P
+
+
+def tile_list_hboth_bias_kernel(tc, xT, w_words, w_scales, wgt, b, wgo, offs, offs2, out):
+    nc = tc.nc
+    with (
+        tc.tile_pool(name="keep", bufs=1) as keep,
+        tc.tile_pool(name="sums", bufs=16) as sums,
+        tc.psum_pool(name="psum", bufs=8) as psum,
+    ):
+        offs_in = keep.tile([P, S // 16], U16, name="offs_in")
+        offs_out = keep.tile([P, S // 16], U16, name="offs_out")
+        wgt_sb = [keep.tile([P, HALF], F32, name=f"wgt{h}") for h in range(2)]
+        wgo_sb = keep.tile([P, S], F32, name="wgo_sb")
+        planes = [keep.tile([P, T], F32, name=f"plane{i}") for i in range(PLANES)]
+        w_sb = keep.tile([P, M], U32, name="w_sb", align_bytes=256)
+        ws_sb = keep.tile([P, M], U8, name="ws_sb", align_bytes=256)
+        b_rows = keep.tile([P, P], F32, name="b_rows")
+        ident = keep.tile([P, P], F32, name="ident")
+        b_cols = keep.tile([P, N_TILES], F32, name="b_cols")
+        warm = keep.tile([P, 1], F32, name="warm")
+        windows = [keep.tile([P, T], F32, name=f"window{m}") for m in range(N_TILES)]
+        picked = [keep.tile([P, PLANES, HALF], F32, name=f"picked{h}") for h in range(2)]
+        grouped = [keep.tile([P, HALF, PLANES], BF16, name=f"grouped{h}", align_bytes=256) for h in range(2)]
+        codes = [keep.tile([P, HALF], U32, name=f"codes{h}", align_bytes=256) for h in range(2)]
+        scales = [keep.tile([P, HALF], U8, name=f"scales{h}", align_bytes=256) for h in range(2)]
+
+        x_view = xT.rearrange("(p i) t -> p i t", i=PLANES)
+        nc.sync.dma_start(offs_in[:], offs)
+        nc.scalar.dma_start(out=wgt_sb[0][:], in_=wgt[:, 0:HALF])
+        nc.sync.dma_start(out=planes[0][:], in_=x_view[:, 0, :])
+        nc.scalar.dma_start(out=wgt_sb[1][:], in_=wgt[:, HALF:S])
+        for i in range(1, PLANES):
+            nc.sync.dma_start(out=planes[i][:], in_=x_view[:, i, :])
+
+        nc.vector.memset(warm[:], 0.0)
+        nc.scalar.activation(warm[:], warm[:], IDENTITY, bias=warm[:, 0:1])
+
+        nc.gpsimd.memset(ws_sb[:].bitcast(I32), 0)
+        nc.gpsimd.memset(b_rows[:], 0.0)
+        make_identity(nc, ident[:])
+        for q in range(4):
+            nc.sync.dma_start(
+                out=ws_sb[32 * q : 32 * q + 4, :].bitcast(I32), in_=w_scales[0, 4 * q : 4 * q + 4, :].bitcast(I32)
+            )
+        nc.sync.dma_start(out=b_rows[0:N_TILES, :], in_=b.rearrange("(m p) -> m p", p=P))
+        for c in range(2):
+            cols = slice(c * M // 2, (c + 1) * M // 2)
+            nc.sync.dma_start(
+                out=w_sb[:, cols].bitcast(I32), in_=w_words[0, :, cols, :].rearrange("p n t -> p (n t)").bitcast(I32)
+            )
+        nc.sync.dma_start(offs_out[:], offs2)
+        nc.sync.dma_start(out=wgo_sb[:], in_=wgo)
+
+        for m in range(5):
+            nc.vector.memset(windows[m][:], 0.0)
+        for m in range(5, N_TILES):
+            nc.gpsimd.memset(windows[m][:], 0.0)
+
+        b_psum = psum.tile([P, S], F32, name="b_psum", tag="acc")
+        nc.tensor.transpose(b_psum[:, 0:P], b_rows[:], ident[:])
+        nc.scalar.copy(out=b_cols[:], in_=b_psum[:, 0:N_TILES])
+
+        half_cols = HALF // 16
+
+        def gather(h, i):
+            nc.vector.tensor_tensor(
+                picked[h][:, i, :],
+                planes[i][:].indirect(offs_in[:, h * half_cols : (h + 1) * half_cols]),
+                wgt_sb[h][:],
+                MULT,
+            )
+
+        def interleave(engine_copy, h):
+            engine_copy(out=grouped[h][:], in_=picked[h][:].rearrange("p i w -> p w i"))
+
+        def quantise(h):
+            nc.vector.quantize_mx(
+                out=codes[h][:].bitcast(FP8X4), scales=scales[h][:], in_=grouped[h][:].rearrange("p w i -> p (w i)")
+            )
+
+        accs = [None] * N_TILES
+        results = {}
+
+        def project(h, m):
+            if h == 0:
+                acc = psum.tile([P, S], F32, name=f"acc{m}", tag="acc")
+                accs[m] = acc
+            cols = slice(m * P, (m + 1) * P)
+            part = accs[m][:, h * HALF : (h + 1) * HALF]
+            nc.tensor.matmul_mx(
+                out=part,
+                lhsT=w_sb[:, cols].bitcast(FP8X4),
+                lhsT_scale=ws_sb[:, cols],
+                rhs=codes[h][:].bitcast(FP8X4),
+                rhs_scale=scales[h][:],
+                start=True,
+                stop=True,
+            )
+            y = sums.tile([P, HALF], F32, name=f"y{h}_{m}", tag="y")
+            nc.scalar.activation(y[:], part, IDENTITY, bias=b_cols[:, m : m + 1])
+            results[(h, m)] = y
+
+        def scatter(h, m):
+            nc.vector.tensor_tensor(
+                windows[m][:].indirect(offs_out[:, h * half_cols : (h + 1) * half_cols]),
+                results[(h, m)][:],
+                wgo_sb[:, h * HALF : (h + 1) * HALF],
+                MULT,
+            )
+
+        gather(0, 0)
+        gather(1, 0)
+        gather(0, 1)
+        gather(1, 1)
+        gather(0, 2)
+        gather(0, 3)
+        interleave(nc.vector.tensor_copy, 0)
+        gather(1, 2)
+        quantise(0)
+        gather(1, 3)
+        for m in range(N_TILES):
+            project(0, m)
+            if m == 0:
+                interleave(nc.scalar.copy, 1)
+        scatter(0, 0)
+        scatter(0, 1)
+        quantise(1)
+        for m in range(2, N_TILES):
+            scatter(0, m)
+        for m in range(N_TILES):
+            project(1, m)
+        for m in range(N_TILES):
+            scatter(1, m)
+            nc.sync.dma_start(out=out[m * P : (m + 1) * P, :], in_=windows[m][:])

@@ -16,20 +16,22 @@ IDENTITY = mybir.ActivationFunctionType.Identity
 
 P = 128
 PLANES = 4
-HALF = S // 2
+LEAD = 128
+REST = S - LEAD
 N_TILES = M // P
+SPLIT_TILES = 3
+EARLY = 4
 
 
 def tile_list_hboth_bias_kernel(tc, xT, w_words, w_scales, wgt, b, wgo, offs, offs2, out):
     nc = tc.nc
     with (
         tc.tile_pool(name="keep", bufs=1) as keep,
-        tc.tile_pool(name="sums", bufs=16) as sums,
         tc.psum_pool(name="psum", bufs=8) as psum,
     ):
         offs_in = keep.tile([P, S // 16], U16, name="offs_in")
         offs_out = keep.tile([P, S // 16], U16, name="offs_out")
-        wgt_sb = [keep.tile([P, HALF], F32, name=f"wgt{h}") for h in range(2)]
+        wgt_sb = keep.tile([P, S], F32, name="wgt_sb")
         wgo_sb = keep.tile([P, S], F32, name="wgo_sb")
         planes = [keep.tile([P, T], F32, name=f"plane{i}") for i in range(PLANES)]
         w_sb = keep.tile([P, M], U32, name="w_sb", align_bytes=256)
@@ -38,117 +40,126 @@ def tile_list_hboth_bias_kernel(tc, xT, w_words, w_scales, wgt, b, wgo, offs, of
         ident = keep.tile([P, P], F32, name="ident")
         b_cols = keep.tile([P, N_TILES], F32, name="b_cols")
         warm = keep.tile([P, 1], F32, name="warm")
-        windows = [keep.tile([P, T], F32, name=f"window{m}") for m in range(N_TILES)]
-        picked = [keep.tile([P, PLANES, HALF], F32, name=f"picked{h}") for h in range(2)]
-        grouped = [keep.tile([P, HALF, PLANES], BF16, name=f"grouped{h}", align_bytes=256) for h in range(2)]
-        codes = [keep.tile([P, HALF], U32, name=f"codes{h}", align_bytes=256) for h in range(2)]
-        scales = [keep.tile([P, HALF], U8, name=f"scales{h}", align_bytes=256) for h in range(2)]
+        picked_lead = keep.tile([P, PLANES, LEAD], F32, name="picked_lead")
+        picked_rest = keep.tile([P, PLANES, REST], F32, name="picked_rest")
+        codes = keep.tile([P, S], U32, name="codes", align_bytes=256)
+        scales = keep.tile([P, S], U8, name="scales", align_bytes=256)
+
+        def load_w(lo, hi):
+            nc.sync.dma_start(
+                out=w_sb[:, lo:hi].bitcast(I32),
+                in_=w_words[0, :, lo:hi, :].rearrange("p n t -> p (n t)").bitcast(I32),
+            )
+
+        nc.gpsimd.memset(b_rows[:], 0.0)
+        nc.gpsimd.memset(ws_sb[:].bitcast(I32), 0)
+        make_identity(nc, ident[:])
 
         x_view = xT.rearrange("(p i) t -> p i t", i=PLANES)
         nc.sync.dma_start(offs_in[:], offs)
-        nc.scalar.dma_start(out=wgt_sb[0][:], in_=wgt[:, 0:HALF])
-        nc.sync.dma_start(out=planes[0][:], in_=x_view[:, 0, :])
-        nc.scalar.dma_start(out=wgt_sb[1][:], in_=wgt[:, HALF:S])
-        for i in range(1, PLANES):
+        nc.scalar.dma_start(out=wgt_sb[:], in_=wgt)
+        for i in range(PLANES):
             nc.sync.dma_start(out=planes[i][:], in_=x_view[:, i, :])
-
-        nc.vector.memset(warm[:], 0.0)
-        nc.scalar.activation(warm[:], warm[:], IDENTITY, bias=warm[:, 0:1])
-
-        nc.gpsimd.memset(ws_sb[:].bitcast(I32), 0)
-        nc.gpsimd.memset(b_rows[:], 0.0)
-        make_identity(nc, ident[:])
+        nc.scalar.dma_start(out=b_rows[0:N_TILES, :], in_=b.rearrange("(m p) -> m p", p=P))
         for q in range(4):
             nc.sync.dma_start(
                 out=ws_sb[32 * q : 32 * q + 4, :].bitcast(I32), in_=w_scales[0, 4 * q : 4 * q + 4, :].bitcast(I32)
             )
-        nc.sync.dma_start(out=b_rows[0:N_TILES, :], in_=b.rearrange("(m p) -> m p", p=P))
-        for c in range(2):
-            cols = slice(c * M // 2, (c + 1) * M // 2)
-            nc.sync.dma_start(
-                out=w_sb[:, cols].bitcast(I32), in_=w_words[0, :, cols, :].rearrange("p n t -> p (n t)").bitcast(I32)
-            )
-        nc.sync.dma_start(offs_out[:], offs2)
+        load_w(0, SPLIT_TILES * P)
         nc.sync.dma_start(out=wgo_sb[:], in_=wgo)
+        nc.sync.dma_start(offs_out[:], offs2)
+        load_w(SPLIT_TILES * P, M)
 
-        for m in range(5):
-            nc.vector.memset(windows[m][:], 0.0)
-        for m in range(5, N_TILES):
-            nc.gpsimd.memset(windows[m][:], 0.0)
+        nc.vector.memset(warm[:], 0.0)
+        nc.scalar.activation(warm[:], warm[:], IDENTITY, bias=warm[:, 0:1])
+
+        windows = {}
+        for m in range(EARLY):
+            windows[m] = keep.tile([P, T], F32, name=f"window{m}")
+            engine = nc.vector if m < 2 else nc.gpsimd
+            engine.memset(windows[m][:], 0.0)
 
         b_psum = psum.tile([P, S], F32, name="b_psum", tag="acc")
         nc.tensor.transpose(b_psum[:, 0:P], b_rows[:], ident[:])
         nc.scalar.copy(out=b_cols[:], in_=b_psum[:, 0:N_TILES])
 
-        half_cols = HALF // 16
-
-        def gather(h, i):
+        def gather(picked, i, lo, hi):
             nc.vector.tensor_tensor(
-                picked[h][:, i, :],
-                planes[i][:].indirect(offs_in[:, h * half_cols : (h + 1) * half_cols]),
-                wgt_sb[h][:],
-                MULT,
+                picked[:, i, :], planes[i][:].indirect(offs_in[:, lo // 16 : hi // 16]), wgt_sb[:, lo:hi], MULT
             )
 
-        def interleave(engine_copy, h):
-            engine_copy(out=grouped[h][:], in_=picked[h][:].rearrange("p i w -> p w i"))
+        def interleave(engine_copy, picked, width):
+            grouped = keep.tile([P, width, PLANES], BF16, name="grouped", tag="grouped", align_bytes=256)
+            engine_copy(
+                out=grouped[:].rearrange("p (c e) i -> p c i e", e=2),
+                in_=picked[:].rearrange("p i (c e) -> p c i e", e=2),
+            )
+            return grouped
 
-        def quantise(h):
+        def quantise(grouped, first, lo, hi):
             nc.vector.quantize_mx(
-                out=codes[h][:].bitcast(FP8X4), scales=scales[h][:], in_=grouped[h][:].rearrange("p w i -> p (w i)")
+                out=codes[:, lo:hi].bitcast(FP8X4),
+                scales=scales[:, lo:hi],
+                in_=grouped[:].rearrange("p w i -> p (w i)")[:, (lo - first) * PLANES : (hi - first) * PLANES],
             )
 
-        accs = [None] * N_TILES
-        results = {}
+        accs = {}
 
-        def project(h, m):
-            if h == 0:
-                acc = psum.tile([P, S], F32, name=f"acc{m}", tag="acc")
-                accs[m] = acc
+        def product(m, lo, hi):
+            if m not in accs:
+                accs[m] = psum.tile([P, S], F32, name=f"acc{m}", tag="acc")
             cols = slice(m * P, (m + 1) * P)
-            part = accs[m][:, h * HALF : (h + 1) * HALF]
             nc.tensor.matmul_mx(
-                out=part,
+                out=accs[m][:, lo:hi],
                 lhsT=w_sb[:, cols].bitcast(FP8X4),
                 lhsT_scale=ws_sb[:, cols],
-                rhs=codes[h][:].bitcast(FP8X4),
-                rhs_scale=scales[h][:],
+                rhs=codes[:, lo:hi].bitcast(FP8X4),
+                rhs_scale=scales[:, lo:hi],
                 start=True,
                 stop=True,
             )
-            y = sums.tile([P, HALF], F32, name=f"y{h}_{m}", tag="y")
-            nc.scalar.activation(y[:], part, IDENTITY, bias=b_cols[:, m : m + 1])
-            results[(h, m)] = y
 
-        def scatter(h, m):
+        def add_bias(m, lo, hi, tag):
+            y = keep.tile([P, hi - lo], F32, name=tag, tag=tag)
+            nc.scalar.activation(y[:], accs[m][:, lo:hi], IDENTITY, bias=b_cols[:, m : m + 1])
+            return y
+
+        def scatter(m, y, lo, hi):
             nc.vector.tensor_tensor(
-                windows[m][:].indirect(offs_out[:, h * half_cols : (h + 1) * half_cols]),
-                results[(h, m)][:],
-                wgo_sb[:, h * HALF : (h + 1) * HALF],
-                MULT,
+                windows[m][:].indirect(offs_out[:, lo // 16 : hi // 16]), y[:], wgo_sb[:, lo:hi], MULT
             )
 
-        gather(0, 0)
-        gather(1, 0)
-        gather(0, 1)
-        gather(1, 1)
-        gather(0, 2)
-        gather(0, 3)
-        interleave(nc.vector.tensor_copy, 0)
-        gather(1, 2)
-        quantise(0)
-        gather(1, 3)
-        for m in range(N_TILES):
-            project(0, m)
-            if m == 0:
-                interleave(nc.scalar.copy, 1)
-        scatter(0, 0)
-        scatter(0, 1)
-        quantise(1)
-        for m in range(2, N_TILES):
-            scatter(0, m)
-        for m in range(N_TILES):
-            project(1, m)
-        for m in range(N_TILES):
-            scatter(1, m)
+        def finish(m, y, lo):
+            scatter(m, y, lo, S)
             nc.sync.dma_start(out=out[m * P : (m + 1) * P, :], in_=windows[m][:])
+            late = m + EARLY
+            if late < N_TILES:
+                windows[late] = keep.tile([P, T], F32, name=f"window{late}", tag=f"tail{m}")
+                nc.gpsimd.memset(windows[late][:], 0.0)
+
+        for i in range(PLANES):
+            gather(picked_lead, i, 0, LEAD)
+            gather(picked_rest, i, LEAD, S)
+        grouped = interleave(nc.scalar.copy, picked_lead, LEAD)
+        quantise(grouped, 0, 0, LEAD)
+        leads = []
+        for m in range(SPLIT_TILES):
+            product(m, 0, LEAD)
+            leads.append(add_bias(m, 0, LEAD, f"lead{m}"))
+        grouped = interleave(nc.vector.tensor_copy, picked_rest, REST)
+        scatter(0, leads[0], 0, LEAD)
+        quantise(grouped, LEAD, LEAD, LEAD + 256)
+        quantise(grouped, LEAD, LEAD + 256, S)
+        for m in range(1, SPLIT_TILES):
+            scatter(m, leads[m], 0, LEAD)
+        tails = []
+        for m in range(N_TILES):
+            if m < SPLIT_TILES:
+                product(m, LEAD, LEAD + 256)
+                product(m, LEAD + 256, S)
+                tails.append(add_bias(m, LEAD, S, f"tail{m}"))
+            else:
+                product(m, 0, S)
+                tails.append(add_bias(m, 0, S, f"tail{m}"))
+        for m in range(N_TILES):
+            finish(m, tails[m], LEAD if m < SPLIT_TILES else 0)

@@ -17,7 +17,7 @@ IDENTITY = mybir.ActivationFunctionType.Identity
 P = 128
 PLANES = 4
 LEAD = 128
-REST = S - LEAD
+MID = 2 * LEAD
 N_TILES = M // P
 SPLIT_TILES = 3
 EARLY = 4
@@ -40,8 +40,7 @@ def tile_list_hboth_bias_kernel(tc, xT, w_words, w_scales, wgt, b, wgo, offs, of
         ident = keep.tile([P, P], F32, name="ident")
         b_cols = keep.tile([P, N_TILES], F32, name="b_cols")
         warm = keep.tile([P, 1], F32, name="warm")
-        picked_lead = keep.tile([P, PLANES, LEAD], F32, name="picked_lead")
-        picked_rest = keep.tile([P, PLANES, REST], F32, name="picked_rest")
+        picked = keep.tile([P, PLANES, S], F32, name="picked")
         codes = keep.tile([P, S], U32, name="codes", align_bytes=256)
         scales = keep.tile([P, S], U8, name="scales", align_bytes=256)
 
@@ -57,17 +56,19 @@ def tile_list_hboth_bias_kernel(tc, xT, w_words, w_scales, wgt, b, wgo, offs, of
 
         x_view = xT.rearrange("(p i) t -> p i t", i=PLANES)
         nc.sync.dma_start(offs_in[:], offs)
-        nc.scalar.dma_start(out=wgt_sb[:], in_=wgt)
-        for i in range(PLANES):
+        nc.scalar.dma_start(out=wgt_sb[:, 0:MID], in_=wgt[:, 0:MID])
+        nc.sync.dma_start(out=planes[0][:], in_=x_view[:, 0, :])
+        nc.sync.dma_start(out=wgt_sb[:, MID:S], in_=wgt[:, MID:S])
+        nc.sync.dma_start(out=b_rows[0:N_TILES, :], in_=b.rearrange("(m p) -> m p", p=P))
+        for i in range(1, PLANES):
             nc.sync.dma_start(out=planes[i][:], in_=x_view[:, i, :])
-        nc.scalar.dma_start(out=b_rows[0:N_TILES, :], in_=b.rearrange("(m p) -> m p", p=P))
+        nc.sync.dma_start(offs_out[:], offs2)
         for q in range(4):
             nc.sync.dma_start(
                 out=ws_sb[32 * q : 32 * q + 4, :].bitcast(I32), in_=w_scales[0, 4 * q : 4 * q + 4, :].bitcast(I32)
             )
         load_w(0, SPLIT_TILES * P)
         nc.sync.dma_start(out=wgo_sb[:], in_=wgo)
-        nc.sync.dma_start(offs_out[:], offs2)
         load_w(SPLIT_TILES * P, M)
 
         nc.vector.memset(warm[:], 0.0)
@@ -83,24 +84,24 @@ def tile_list_hboth_bias_kernel(tc, xT, w_words, w_scales, wgt, b, wgo, offs, of
         nc.tensor.transpose(b_psum[:, 0:P], b_rows[:], ident[:])
         nc.scalar.copy(out=b_cols[:], in_=b_psum[:, 0:N_TILES])
 
-        def gather(picked, i, lo, hi):
+        def gather(i, lo, hi):
             nc.vector.tensor_tensor(
-                picked[:, i, :], planes[i][:].indirect(offs_in[:, lo // 16 : hi // 16]), wgt_sb[:, lo:hi], MULT
+                picked[:, i, lo:hi], planes[i][:].indirect(offs_in[:, lo // 16 : hi // 16]), wgt_sb[:, lo:hi], MULT
             )
 
-        def interleave(engine_copy, picked, width):
-            grouped = keep.tile([P, width, PLANES], BF16, name="grouped", tag="grouped", align_bytes=256)
+        def interleave(engine_copy, lo, hi, tag):
+            grouped = keep.tile([P, hi - lo, PLANES], BF16, name=tag, tag=tag, align_bytes=256)
             engine_copy(
                 out=grouped[:].rearrange("p (c e) i -> p c i e", e=2),
-                in_=picked[:].rearrange("p i (c e) -> p c i e", e=2),
+                in_=picked[:, :, lo:hi].rearrange("p i (c e) -> p c i e", e=2),
             )
             return grouped
 
-        def quantise(grouped, first, lo, hi):
+        def quantise(grouped, lo, hi):
             nc.vector.quantize_mx(
                 out=codes[:, lo:hi].bitcast(FP8X4),
                 scales=scales[:, lo:hi],
-                in_=grouped[:].rearrange("p w i -> p (w i)")[:, (lo - first) * PLANES : (hi - first) * PLANES],
+                in_=grouped[:].rearrange("p w i -> p (w i)"),
             )
 
         accs = {}
@@ -137,26 +138,32 @@ def tile_list_hboth_bias_kernel(tc, xT, w_words, w_scales, wgt, b, wgo, offs, of
                 windows[late] = keep.tile([P, T], F32, name=f"window{late}", tag=f"tail{m}")
                 nc.gpsimd.memset(windows[late][:], 0.0)
 
-        for i in range(PLANES):
-            gather(picked_lead, i, 0, LEAD)
-            gather(picked_rest, i, LEAD, S)
-        grouped = interleave(nc.scalar.copy, picked_lead, LEAD)
-        quantise(grouped, 0, 0, LEAD)
+        last = PLANES - 1
+        gather(0, 0, MID)
+        gather(0, MID, S)
+        for i in range(1, last):
+            gather(i, 0, S)
+        gather(last, 0, LEAD)
+        gather(last, LEAD, MID)
+        gather(last, MID, S)
+        grouped_lead = interleave(nc.scalar.copy, 0, LEAD, "grouped")
+        grouped_mid = interleave(nc.scalar.copy, LEAD, MID, "grouped_mid")
+        quantise(grouped_lead, 0, LEAD)
         leads = []
         for m in range(SPLIT_TILES):
             product(m, 0, LEAD)
             leads.append(add_bias(m, 0, LEAD, f"lead{m}"))
-        grouped = interleave(nc.vector.tensor_copy, picked_rest, REST)
+        grouped_last = interleave(nc.vector.tensor_copy, MID, S, "grouped")
+        quantise(grouped_mid, LEAD, MID)
+        quantise(grouped_last, MID, S)
         scatter(0, leads[0], 0, LEAD)
-        quantise(grouped, LEAD, LEAD, LEAD + 256)
-        quantise(grouped, LEAD, LEAD + 256, S)
         for m in range(1, SPLIT_TILES):
             scatter(m, leads[m], 0, LEAD)
         tails = []
         for m in range(N_TILES):
             if m < SPLIT_TILES:
-                product(m, LEAD, LEAD + 256)
-                product(m, LEAD + 256, S)
+                product(m, LEAD, MID)
+                product(m, MID, S)
                 tails.append(add_bias(m, LEAD, S, f"tail{m}"))
             else:
                 product(m, 0, S)

@@ -18,6 +18,7 @@ P = 128
 PLANES = 4
 LEAD = 128
 MID = 2 * LEAD
+LAST = 3 * LEAD
 N_TILES = M // P
 SPLIT_TILES = 3
 EARLY = 4
@@ -55,9 +56,9 @@ def tile_list_hboth_bias_kernel(tc, xT, w_words, w_scales, wgt, b, wgo, offs, of
         make_identity(nc, ident[:])
 
         x_view = xT.rearrange("(p i) t -> p i t", i=PLANES)
-        nc.sync.dma_start(offs_in[:], offs)
         nc.scalar.dma_start(out=wgt_sb[:, 0:MID], in_=wgt[:, 0:MID])
         nc.sync.dma_start(out=planes[0][:], in_=x_view[:, 0, :])
+        nc.sync.dma_start(offs_in[:], offs)
         nc.sync.dma_start(out=wgt_sb[:, MID:S], in_=wgt[:, MID:S])
         nc.sync.dma_start(out=b_rows[0:N_TILES, :], in_=b.rearrange("(m p) -> m p", p=P))
         for i in range(1, PLANES):
@@ -89,13 +90,14 @@ def tile_list_hboth_bias_kernel(tc, xT, w_words, w_scales, wgt, b, wgo, offs, of
                 picked[:, i, lo:hi], planes[i][:].indirect(offs_in[:, lo // 16 : hi // 16]), wgt_sb[:, lo:hi], MULT
             )
 
-        def interleave(engine_copy, lo, hi, tag):
-            grouped = keep.tile([P, hi - lo, PLANES], BF16, name=tag, tag=tag, align_bytes=256)
+        def grouped_tile(width, tag):
+            return keep.tile([P, width, PLANES], BF16, name=tag, tag=tag, align_bytes=256)
+
+        def interleave(engine_copy, grouped, first, lo, hi, rows=slice(0, PLANES)):
             engine_copy(
-                out=grouped[:].rearrange("p (c e) i -> p c i e", e=2),
-                in_=picked[:, :, lo:hi].rearrange("p i (c e) -> p c i e", e=2),
+                out=grouped[:, lo - first : hi - first, rows].rearrange("p (c e) i -> p c i e", e=2),
+                in_=picked[:, rows, lo:hi].rearrange("p i (c e) -> p c i e", e=2),
             )
-            return grouped
 
         def quantise(grouped, lo, hi):
             nc.vector.quantize_mx(
@@ -146,24 +148,31 @@ def tile_list_hboth_bias_kernel(tc, xT, w_words, w_scales, wgt, b, wgo, offs, of
         gather(last, 0, LEAD)
         gather(last, LEAD, MID)
         gather(last, MID, S)
-        grouped_lead = interleave(nc.scalar.copy, 0, LEAD, "grouped")
-        grouped_mid = interleave(nc.scalar.copy, LEAD, MID, "grouped_mid")
+        grouped_lead = grouped_tile(LEAD, "grouped")
+        grouped_mid = grouped_tile(LAST - LEAD, "grouped_mid")
+        low, high = slice(0, 2), slice(2, PLANES)
+        interleave(nc.scalar.copy, grouped_lead, 0, 0, LEAD, low)
+        interleave(nc.scalar.copy, grouped_mid, LEAD, LEAD, LAST, low)
+        interleave(nc.scalar.copy, grouped_lead, 0, 0, LEAD, high)
+        interleave(nc.scalar.copy, grouped_mid, LEAD, LEAD, MID, high)
+        interleave(nc.scalar.copy, grouped_mid, LEAD, MID, LAST, high)
         quantise(grouped_lead, 0, LEAD)
         leads = []
         for m in range(SPLIT_TILES):
             product(m, 0, LEAD)
             leads.append(add_bias(m, 0, LEAD, f"lead{m}"))
-        grouped_last = interleave(nc.vector.tensor_copy, MID, S, "grouped")
-        quantise(grouped_mid, LEAD, MID)
-        quantise(grouped_last, MID, S)
+        grouped_last = grouped_tile(S - LAST, "grouped")
+        interleave(nc.vector.tensor_copy, grouped_last, LAST, LAST, S)
+        quantise(grouped_last, LAST, S)
+        quantise(grouped_mid, LEAD, LAST)
         scatter(0, leads[0], 0, LEAD)
         for m in range(1, SPLIT_TILES):
             scatter(m, leads[m], 0, LEAD)
         tails = []
         for m in range(N_TILES):
             if m < SPLIT_TILES:
-                product(m, LEAD, MID)
-                product(m, MID, S)
+                product(m, LAST, S)
+                product(m, LEAD, LAST)
                 tails.append(add_bias(m, LEAD, S, f"tail{m}"))
             else:
                 product(m, 0, S)

@@ -16,12 +16,12 @@ IDENTITY = mybir.ActivationFunctionType.Identity
 
 P = 128
 PLANES = 4
-LEAD = 128
-MID = 2 * LEAD
-LAST = 3 * LEAD
+GROUP = 16
 N_TILES = M // P
-SPLIT_TILES = 3
-EARLY = 4
+LEAD, HALF, LAST = S // 4, S // 2, 3 * S // 4
+LEAD_TILES = 3
+EARLY_WINDOWS = 4
+VECTOR_WINDOWS = 2
 
 
 def tile_list_hboth_bias_kernel(tc, xT, w_words, w_scales, wgt, b, wgo, offs, offs2, out):
@@ -30,8 +30,8 @@ def tile_list_hboth_bias_kernel(tc, xT, w_words, w_scales, wgt, b, wgo, offs, of
         tc.tile_pool(name="keep", bufs=1) as keep,
         tc.psum_pool(name="psum", bufs=8) as psum,
     ):
-        offs_in = keep.tile([P, S // 16], U16, name="offs_in")
-        offs_out = keep.tile([P, S // 16], U16, name="offs_out")
+        offs_in = keep.tile([P, S // GROUP], U16, name="offs_in")
+        offs_out = keep.tile([P, S // GROUP], U16, name="offs_out")
         wgt_sb = keep.tile([P, S], F32, name="wgt_sb")
         wgo_sb = keep.tile([P, S], F32, name="wgo_sb")
         planes = [keep.tile([P, T], F32, name=f"plane{i}") for i in range(PLANES)]
@@ -40,7 +40,6 @@ def tile_list_hboth_bias_kernel(tc, xT, w_words, w_scales, wgt, b, wgo, offs, of
         b_rows = keep.tile([P, P], F32, name="b_rows")
         ident = keep.tile([P, P], F32, name="ident")
         b_cols = keep.tile([P, N_TILES], F32, name="b_cols")
-        warm = keep.tile([P, 1], F32, name="warm")
         picked = keep.tile([P, PLANES, S], F32, name="picked")
         codes = keep.tile([P, S], U32, name="codes", align_bytes=256)
         scales = keep.tile([P, S], U8, name="scales", align_bytes=256)
@@ -56,10 +55,10 @@ def tile_list_hboth_bias_kernel(tc, xT, w_words, w_scales, wgt, b, wgo, offs, of
         make_identity(nc, ident[:])
 
         x_view = xT.rearrange("(p i) t -> p i t", i=PLANES)
-        nc.scalar.dma_start(out=wgt_sb[:, 0:MID], in_=wgt[:, 0:MID])
+        nc.scalar.dma_start(out=wgt_sb[:, 0:HALF], in_=wgt[:, 0:HALF])
         nc.sync.dma_start(out=planes[0][:], in_=x_view[:, 0, :])
         nc.sync.dma_start(offs_in[:], offs)
-        nc.sync.dma_start(out=wgt_sb[:, MID:S], in_=wgt[:, MID:S])
+        nc.sync.dma_start(out=wgt_sb[:, HALF:S], in_=wgt[:, HALF:S])
         nc.sync.dma_start(out=b_rows[0:N_TILES, :], in_=b.rearrange("(m p) -> m p", p=P))
         for i in range(1, PLANES):
             nc.sync.dma_start(out=planes[i][:], in_=x_view[:, i, :])
@@ -68,32 +67,32 @@ def tile_list_hboth_bias_kernel(tc, xT, w_words, w_scales, wgt, b, wgo, offs, of
             nc.sync.dma_start(
                 out=ws_sb[32 * q : 32 * q + 4, :].bitcast(I32), in_=w_scales[0, 4 * q : 4 * q + 4, :].bitcast(I32)
             )
-        load_w(0, SPLIT_TILES * P)
+        load_w(0, LEAD_TILES * P)
         nc.sync.dma_start(out=wgo_sb[:], in_=wgo)
-        load_w(SPLIT_TILES * P, M)
-
-        nc.vector.memset(warm[:], 0.0)
-        nc.scalar.activation(warm[:], warm[:], IDENTITY, bias=warm[:, 0:1])
+        load_w(LEAD_TILES * P, M)
 
         windows = {}
-        for m in range(EARLY):
+        for m in range(EARLY_WINDOWS):
             windows[m] = keep.tile([P, T], F32, name=f"window{m}")
-            engine = nc.vector if m < 2 else nc.gpsimd
+            engine = nc.vector if m < VECTOR_WINDOWS else nc.gpsimd
             engine.memset(windows[m][:], 0.0)
 
         b_psum = psum.tile([P, S], F32, name="b_psum", tag="acc")
         nc.tensor.transpose(b_psum[:, 0:P], b_rows[:], ident[:])
-        nc.scalar.copy(out=b_cols[:], in_=b_psum[:, 0:N_TILES])
+        nc.scalar.activation(b_cols[:], b_psum[:, 0:N_TILES], IDENTITY)
 
         def gather(i, lo, hi):
             nc.vector.tensor_tensor(
-                picked[:, i, lo:hi], planes[i][:].indirect(offs_in[:, lo // 16 : hi // 16]), wgt_sb[:, lo:hi], MULT
+                picked[:, i, lo:hi],
+                planes[i][:].indirect(offs_in[:, lo // GROUP : hi // GROUP]),
+                wgt_sb[:, lo:hi],
+                MULT,
             )
 
         def grouped_tile(width, tag):
             return keep.tile([P, width, PLANES], BF16, name=tag, tag=tag, align_bytes=256)
 
-        def interleave(engine_copy, grouped, first, lo, hi, rows=slice(0, PLANES)):
+        def interleave(engine_copy, grouped, first, lo, hi, rows):
             engine_copy(
                 out=grouped[:, lo - first : hi - first, rows].rearrange("p (c e) i -> p c i e", e=2),
                 in_=picked[:, rows, lo:hi].rearrange("p i (c e) -> p c i e", e=2),
@@ -129,53 +128,53 @@ def tile_list_hboth_bias_kernel(tc, xT, w_words, w_scales, wgt, b, wgo, offs, of
 
         def scatter(m, y, lo, hi):
             nc.vector.tensor_tensor(
-                windows[m][:].indirect(offs_out[:, lo // 16 : hi // 16]), y[:], wgo_sb[:, lo:hi], MULT
+                windows[m][:].indirect(offs_out[:, lo // GROUP : hi // GROUP]), y[:], wgo_sb[:, lo:hi], MULT
             )
 
-        def finish(m, y, lo):
-            scatter(m, y, lo, S)
-            nc.sync.dma_start(out=out[m * P : (m + 1) * P, :], in_=windows[m][:])
-            late = m + EARLY
-            if late < N_TILES:
-                windows[late] = keep.tile([P, T], F32, name=f"window{late}", tag=f"tail{m}")
-                nc.gpsimd.memset(windows[late][:], 0.0)
-
-        last = PLANES - 1
-        gather(0, 0, MID)
-        gather(0, MID, S)
-        for i in range(1, last):
+        last_plane = PLANES - 1
+        gather(0, 0, HALF)
+        gather(0, HALF, S)
+        for i in range(1, last_plane):
             gather(i, 0, S)
-        gather(last, 0, LEAD)
-        gather(last, LEAD, MID)
-        gather(last, MID, S)
-        grouped_lead = grouped_tile(LEAD, "grouped")
-        grouped_mid = grouped_tile(LAST - LEAD, "grouped_mid")
-        low, high = slice(0, 2), slice(2, PLANES)
+        gather(last_plane, 0, LEAD)
+        gather(last_plane, LEAD, HALF)
+        gather(last_plane, HALF, S)
+
+        grouped_lead = grouped_tile(LEAD, "grouped_ends")
+        grouped_middle = grouped_tile(LAST - LEAD, "grouped_middle")
+        low, high, every = slice(0, 2), slice(2, PLANES), slice(0, PLANES)
         interleave(nc.scalar.copy, grouped_lead, 0, 0, LEAD, low)
-        interleave(nc.scalar.copy, grouped_mid, LEAD, LEAD, LAST, low)
+        interleave(nc.scalar.copy, grouped_middle, LEAD, LEAD, LAST, low)
         interleave(nc.scalar.copy, grouped_lead, 0, 0, LEAD, high)
-        interleave(nc.scalar.copy, grouped_mid, LEAD, LEAD, MID, high)
-        interleave(nc.scalar.copy, grouped_mid, LEAD, MID, LAST, high)
+        interleave(nc.scalar.copy, grouped_middle, LEAD, LEAD, HALF, high)
+        interleave(nc.scalar.copy, grouped_middle, LEAD, HALF, LAST, high)
         quantise(grouped_lead, 0, LEAD)
         leads = []
-        for m in range(SPLIT_TILES):
+        for m in range(LEAD_TILES):
             product(m, 0, LEAD)
             leads.append(add_bias(m, 0, LEAD, f"lead{m}"))
-        grouped_last = grouped_tile(S - LAST, "grouped")
-        interleave(nc.vector.tensor_copy, grouped_last, LAST, LAST, S)
+
+        grouped_last = grouped_tile(S - LAST, "grouped_ends")
+        interleave(nc.vector.tensor_copy, grouped_last, LAST, LAST, S, every)
         quantise(grouped_last, LAST, S)
-        quantise(grouped_mid, LEAD, LAST)
-        scatter(0, leads[0], 0, LEAD)
-        for m in range(1, SPLIT_TILES):
+        quantise(grouped_middle, LEAD, LAST)
+        for m in range(LEAD_TILES):
             scatter(m, leads[m], 0, LEAD)
-        tails = []
+
+        rests = []
         for m in range(N_TILES):
-            if m < SPLIT_TILES:
+            if m < LEAD_TILES:
                 product(m, LAST, S)
                 product(m, LEAD, LAST)
-                tails.append(add_bias(m, LEAD, S, f"tail{m}"))
+                rests.append(add_bias(m, LEAD, S, f"rest{m}"))
             else:
                 product(m, 0, S)
-                tails.append(add_bias(m, 0, S, f"tail{m}"))
+                rests.append(add_bias(m, 0, S, f"rest{m}"))
+
         for m in range(N_TILES):
-            finish(m, tails[m], LEAD if m < SPLIT_TILES else 0)
+            scatter(m, rests[m], LEAD if m < LEAD_TILES else 0, S)
+            nc.sync.dma_start(out=out[m * P : (m + 1) * P, :], in_=windows[m][:])
+            late = m + EARLY_WINDOWS
+            if late < N_TILES:
+                windows[late] = keep.tile([P, T], F32, name=f"window{late}", tag=f"rest{m}")
+                nc.gpsimd.memset(windows[late][:], 0.0)

@@ -17,11 +17,11 @@ IDENTITY = mybir.ActivationFunctionType.Identity
 P = 128
 PLANES = 4
 GROUP = 16
+BLOCK = 32
 N_TILES = M // P
 LEAD, HALF, LAST = S // 4, S // 2, 3 * S // 4
 LEAD_TILES = 3
 EARLY_WINDOWS = 4
-VECTOR_WINDOWS = 2
 
 
 def tile_list_hboth_bias_kernel(tc, xT, w_words, w_scales, wgt, b, wgo, offs, offs2, out):
@@ -32,7 +32,10 @@ def tile_list_hboth_bias_kernel(tc, xT, w_words, w_scales, wgt, b, wgo, offs, of
     ):
         offs_in = keep.tile([P, S // GROUP], U16, name="offs_in")
         offs_out = keep.tile([P, S // GROUP], U16, name="offs_out")
-        wgt_sb = keep.tile([P, S], F32, name="wgt_sb")
+        wgt_sb = keep.tile([P, S], F32, name="wgt_sb", align_bytes=64)
+        wgt_dealt = keep.tile([P, BLOCK], F32, name="wgt_dealt", align_bytes=64)
+        wgt_turned = keep.tile([P, BLOCK], F32, name="wgt_turned", align_bytes=64)
+        wgt_spread = [keep.tile([P, HALF], F32, name=f"wgt_spread{h}", align_bytes=64) for h in range(2)]
         wgo_sb = keep.tile([P, S], F32, name="wgo_sb")
         planes = [keep.tile([P, T], F32, name=f"plane{i}") for i in range(PLANES)]
         w_sb = keep.tile([P, M], U32, name="w_sb", align_bytes=256)
@@ -55,10 +58,9 @@ def tile_list_hboth_bias_kernel(tc, xT, w_words, w_scales, wgt, b, wgo, offs, of
         make_identity(nc, ident[:])
 
         x_view = xT.rearrange("(p i) t -> p i t", i=PLANES)
-        nc.scalar.dma_start(out=wgt_sb[:, 0:HALF], in_=wgt[:, 0:HALF])
+        nc.sync.dma_start(out=wgt_dealt[:], in_=wgt.rearrange("(g r) (s a) -> r g s a", r=GROUP, a=BLOCK)[0])
         nc.sync.dma_start(out=planes[0][:], in_=x_view[:, 0, :])
         nc.sync.dma_start(offs_in[:], offs)
-        nc.sync.dma_start(out=wgt_sb[:, HALF:S], in_=wgt[:, HALF:S])
         nc.sync.dma_start(out=b_rows[0:N_TILES, :], in_=b.rearrange("(m p) -> m p", p=P))
         for i in range(1, PLANES):
             nc.sync.dma_start(out=planes[i][:], in_=x_view[:, i, :])
@@ -71,11 +73,22 @@ def tile_list_hboth_bias_kernel(tc, xT, w_words, w_scales, wgt, b, wgo, offs, of
         nc.sync.dma_start(out=wgo_sb[:], in_=wgo)
         load_w(LEAD_TILES * P, M)
 
-        windows = {}
-        for m in range(EARLY_WINDOWS):
-            windows[m] = keep.tile([P, T], F32, name=f"window{m}")
-            engine = nc.vector if m < VECTOR_WINDOWS else nc.gpsimd
-            engine.memset(windows[m][:], 0.0)
+        windows = {0: keep.tile([P, T], F32, name="window0")}
+        nc.vector.memset(windows[0][:], 0.0)
+
+        nc.vector.transpose(wgt_turned[:], wgt_dealt[:])
+        turned_view = wgt_turned[:].rearrange("p (h s) -> p s h", h=2)
+        for half in range(2):
+            blocks = slice(half * HALF // BLOCK, (half + 1) * HALF // BLOCK)
+            nc.vector.tensor_copy(
+                out=wgt_spread[half][:].rearrange("p (s h r) -> p s h r", h=2, r=GROUP),
+                in_=turned_view[:, blocks].unsqueeze(3).to_broadcast([P, HALF // BLOCK, 2, GROUP]),
+            )
+        for half in range(2):
+            nc.vector.transpose(wgt_sb[:, half * HALF : (half + 1) * HALF], wgt_spread[half][:])
+        for m, tag in enumerate(("wgt_turned", "wgt_spread0", "wgt_spread1"), start=1):
+            windows[m] = keep.tile([P, T], F32, name=f"window{m}", tag=tag, align_bytes=64)
+            nc.gpsimd.memset(windows[m][:], 0.0)
 
         b_psum = psum.tile([P, S], F32, name="b_psum", tag="acc")
         nc.tensor.transpose(b_psum[:, 0:P], b_rows[:], ident[:])

@@ -17,10 +17,9 @@ IDENTITY = mybir.ActivationFunctionType.Identity
 P = 128
 PLANES = 4
 GROUP = 16
-BLOCK = 32
 N_TILES = M // P
 LEAD, HALF, LAST = S // 4, S // 2, 3 * S // 4
-LEAD_TILES = 3
+LEAD_TILES = 2
 EARLY_WINDOWS = 4
 
 
@@ -32,10 +31,7 @@ def tile_list_hboth_bias_kernel(tc, xT, w_words, w_scales, wgt, b, wgo, offs, of
     ):
         offs_in = keep.tile([P, S // GROUP], U16, name="offs_in")
         offs_out = keep.tile([P, S // GROUP], U16, name="offs_out")
-        wgt_sb = keep.tile([P, S], F32, name="wgt_sb", align_bytes=64)
-        wgt_dealt = keep.tile([P, BLOCK], F32, name="wgt_dealt", align_bytes=64)
-        wgt_turned = keep.tile([P, BLOCK], F32, name="wgt_turned", align_bytes=64)
-        wgt_spread = [keep.tile([P, HALF], F32, name=f"wgt_spread{h}", align_bytes=64) for h in range(2)]
+        wgt_sb = keep.tile([P, S], F32, name="wgt_sb")
         wgo_sb = keep.tile([P, S], F32, name="wgo_sb")
         planes = [keep.tile([P, T], F32, name=f"plane{i}") for i in range(PLANES)]
         w_sb = keep.tile([P, M], U32, name="w_sb", align_bytes=256)
@@ -58,9 +54,10 @@ def tile_list_hboth_bias_kernel(tc, xT, w_words, w_scales, wgt, b, wgo, offs, of
         make_identity(nc, ident[:])
 
         x_view = xT.rearrange("(p i) t -> p i t", i=PLANES)
-        nc.sync.dma_start(out=wgt_dealt[:], in_=wgt.rearrange("(g r) (s a) -> r g s a", r=GROUP, a=BLOCK)[0])
+        nc.scalar.dma_start(out=wgt_sb[:, 0:HALF], in_=wgt[:, 0:HALF])
         nc.sync.dma_start(out=planes[0][:], in_=x_view[:, 0, :])
         nc.sync.dma_start(offs_in[:], offs)
+        nc.sync.dma_start(out=wgt_sb[:, HALF:S], in_=wgt[:, HALF:S])
         nc.sync.dma_start(out=b_rows[0:N_TILES, :], in_=b.rearrange("(m p) -> m p", p=P))
         for i in range(1, PLANES):
             nc.sync.dma_start(out=planes[i][:], in_=x_view[:, i, :])
@@ -73,26 +70,18 @@ def tile_list_hboth_bias_kernel(tc, xT, w_words, w_scales, wgt, b, wgo, offs, of
         nc.sync.dma_start(out=wgo_sb[:], in_=wgo)
         load_w(LEAD_TILES * P, M)
 
-        windows = {0: keep.tile([P, T], F32, name="window0")}
-        nc.vector.memset(windows[0][:], 0.0)
-
-        nc.vector.transpose(wgt_turned[:], wgt_dealt[:])
-        turned_view = wgt_turned[:].rearrange("p (h s) -> p s h", h=2)
-        for half in range(2):
-            blocks = slice(half * HALF // BLOCK, (half + 1) * HALF // BLOCK)
-            nc.vector.tensor_copy(
-                out=wgt_spread[half][:].rearrange("p (s h r) -> p s h r", h=2, r=GROUP),
-                in_=turned_view[:, blocks].unsqueeze(3).to_broadcast([P, HALF // BLOCK, 2, GROUP]),
-            )
-        for half in range(2):
-            nc.vector.transpose(wgt_sb[:, half * HALF : (half + 1) * HALF], wgt_spread[half][:])
-        for m, tag in enumerate(("wgt_turned", "wgt_spread0", "wgt_spread1"), start=1):
-            windows[m] = keep.tile([P, T], F32, name=f"window{m}", tag=tag, align_bytes=64)
-            nc.gpsimd.memset(windows[m][:], 0.0)
+        windows = {}
+        for m in range(LEAD_TILES):
+            windows[m] = keep.tile([P, T], F32, name=f"window{m}")
+            nc.vector.memset(windows[m][:], 0.0)
 
         b_psum = psum.tile([P, S], F32, name="b_psum", tag="acc")
         nc.tensor.transpose(b_psum[:, 0:P], b_rows[:], ident[:])
         nc.scalar.activation(b_cols[:], b_psum[:, 0:N_TILES], IDENTITY)
+
+        for m, tag in enumerate(("b_rows", "ident"), start=LEAD_TILES):
+            windows[m] = keep.tile([P, T], F32, name=f"window{m}", tag=tag)
+            nc.gpsimd.memset(windows[m][:], 0.0)
 
         def gather(i, lo, hi):
             nc.vector.tensor_tensor(
@@ -118,14 +107,10 @@ def tile_list_hboth_bias_kernel(tc, xT, w_words, w_scales, wgt, b, wgo, offs, of
                 in_=grouped[:].rearrange("p w i -> p (w i)"),
             )
 
-        accs = {}
-
-        def product(m, lo, hi):
-            if m not in accs:
-                accs[m] = psum.tile([P, S], F32, name=f"acc{m}", tag="acc")
+        def product(acc, m, lo, hi):
             cols = slice(m * P, (m + 1) * P)
             nc.tensor.matmul_mx(
-                out=accs[m][:, lo:hi],
+                out=acc[:, lo:hi],
                 lhsT=w_sb[:, cols].bitcast(FP8X4),
                 lhsT_scale=ws_sb[:, cols],
                 rhs=codes[:, lo:hi].bitcast(FP8X4),
@@ -134,10 +119,8 @@ def tile_list_hboth_bias_kernel(tc, xT, w_words, w_scales, wgt, b, wgo, offs, of
                 stop=True,
             )
 
-        def add_bias(m, lo, hi, tag):
-            y = keep.tile([P, hi - lo], F32, name=tag, tag=tag)
-            nc.scalar.activation(y[:], accs[m][:, lo:hi], IDENTITY, bias=b_cols[:, m : m + 1])
-            return y
+        def add_bias(y, acc, m, lo, hi):
+            nc.scalar.activation(y, acc[:, lo:hi], IDENTITY, bias=b_cols[:, m : m + 1])
 
         def scatter(m, y, lo, hi):
             nc.vector.tensor_tensor(
@@ -164,8 +147,11 @@ def tile_list_hboth_bias_kernel(tc, xT, w_words, w_scales, wgt, b, wgo, offs, of
         quantise(grouped_lead, 0, LEAD)
         leads = []
         for m in range(LEAD_TILES):
-            product(m, 0, LEAD)
-            leads.append(add_bias(m, 0, LEAD, f"lead{m}"))
+            acc = psum.tile([P, S], F32, name=f"lead_acc{m}", tag="acc")
+            lead = keep.tile([P, LEAD], F32, name=f"lead{m}")
+            product(acc, m, 0, LEAD)
+            add_bias(lead[:], acc, m, 0, LEAD)
+            leads.append(lead)
 
         grouped_last = grouped_tile(S - LAST, "grouped_ends")
         interleave(nc.vector.tensor_copy, grouped_last, LAST, LAST, S, every)
@@ -176,13 +162,22 @@ def tile_list_hboth_bias_kernel(tc, xT, w_words, w_scales, wgt, b, wgo, offs, of
 
         rests = []
         for m in range(N_TILES):
-            if m < LEAD_TILES:
-                product(m, LAST, S)
-                product(m, LEAD, LAST)
-                rests.append(add_bias(m, LEAD, S, f"rest{m}"))
+            lo = LEAD if m < LEAD_TILES else 0
+            rest = keep.tile([P, S - lo], F32, name=f"rest{m}", tag=f"rest{m}")
+            if m == 0:
+                for part_lo, part_hi in ((LAST, S), (LEAD, LAST)):
+                    part_acc = psum.tile([P, S], F32, name=f"part_acc{part_lo}", tag="acc")
+                    product(part_acc, m, part_lo, part_hi)
+                    add_bias(rest[:, part_lo - lo : part_hi - lo], part_acc, m, part_lo, part_hi)
             else:
-                product(m, 0, S)
-                rests.append(add_bias(m, 0, S, f"rest{m}"))
+                acc = psum.tile([P, S], F32, name=f"acc{m}", tag="acc")
+                if m < LEAD_TILES:
+                    product(acc, m, LAST, S)
+                    product(acc, m, LEAD, LAST)
+                else:
+                    product(acc, m, 0, S)
+                add_bias(rest[:], acc, m, lo, S)
+            rests.append(rest)
 
         for m in range(N_TILES):
             scatter(m, rests[m], LEAD if m < LEAD_TILES else 0, S)

@@ -124,7 +124,7 @@ def tile_list_hboth_bias_kernel(tc, xT, w_words, w_scales, wgt, b, wgo, offs, of
 
         def scatter(m, y, lo, hi):
             nc.vector.tensor_tensor(
-                windows[m][:].indirect(offs_out[:, lo // GROUP : hi // GROUP]), y[:], wgo_sb[:, lo:hi], MULT
+                windows[m % EARLY_WINDOWS][:].indirect(offs_out[:, lo // GROUP : hi // GROUP]), y[:], wgo_sb[:, lo:hi], MULT
             )
 
         last_plane = PLANES - 1
@@ -181,8 +181,4 @@ def tile_list_hboth_bias_kernel(tc, xT, w_words, w_scales, wgt, b, wgo, offs, of
 
         for m in range(N_TILES):
             scatter(m, rests[m], LEAD if m < LEAD_TILES else 0, S)
-            nc.sync.dma_start(out=out[m * P : (m + 1) * P, :], in_=windows[m][:])
-            late = m + EARLY_WINDOWS
-            if late < N_TILES:
-                windows[late] = keep.tile([P, T], F32, name=f"window{late}", tag=f"rest{m}")
-                nc.gpsimd.memset(windows[late][:], 0.0)
+            nc.sync.dma_start(out=out[m * P : (m + 1) * P, :], in_=windows[m % EARLY_WINDOWS][:])

@@ -21,6 +21,7 @@ N_TILES = M // P
 LEAD, HALF, LAST = S // 4, S // 2, 3 * S // 4
 LEAD_TILES = 2
 EARLY_WINDOWS = 4
+PITCH = S + LEAD
 
 
 def tile_list_hboth_bias_kernel(tc, xT, w_words, w_scales, wgt, b, wgo, offs, offs2, out):
@@ -39,7 +40,9 @@ def tile_list_hboth_bias_kernel(tc, xT, w_words, w_scales, wgt, b, wgo, offs, of
         b_rows = keep.tile([P, P], F32, name="b_rows")
         ident = keep.tile([P, P], F32, name="ident")
         b_cols = keep.tile([P, N_TILES], F32, name="b_cols")
-        picked = keep.tile([P, PLANES, S], F32, name="picked")
+        picked = keep.tile([P, PLANES * PITCH], F32, name="picked", align_bytes=256)
+        by_plane = picked[:].rearrange("p (i c) -> p i c", i=PLANES)
+        lead_high = picked[:, 2 * PITCH - LEAD : 2 * PITCH + LEAD]
         codes = keep.tile([P, S], U32, name="codes", align_bytes=256)
         scales = keep.tile([P, S], U8, name="scales", align_bytes=256)
 
@@ -83,28 +86,28 @@ def tile_list_hboth_bias_kernel(tc, xT, w_words, w_scales, wgt, b, wgo, offs, of
             windows[m] = keep.tile([P, T], F32, name=f"window{m}", tag=tag)
             nc.gpsimd.memset(windows[m][:], 0.0)
 
-        def gather(i, lo, hi):
+        def gather(i, lo, hi, dst=None):
             nc.vector.tensor_tensor(
-                picked[:, i, lo:hi],
+                picked[:, i * PITCH + lo : i * PITCH + hi] if dst is None else dst,
                 planes[i][:].indirect(offs_in[:, lo // GROUP : hi // GROUP]),
                 wgt_sb[:, lo:hi],
                 MULT,
             )
 
         def grouped_tile(width, tag):
-            return keep.tile([P, width, PLANES], BF16, name=tag, tag=tag, align_bytes=256)
+            return keep.tile([P, width, PLANES], BF16, name=tag, tag=tag, align_bytes=256)[:]
 
-        def interleave(engine_copy, grouped, first, lo, hi, rows):
+        def interleave(engine_copy, grouped, first, lo, hi, rows, src=None):
             engine_copy(
                 out=grouped[:, lo - first : hi - first, rows].rearrange("p (c e) i -> p c i e", e=2),
-                in_=picked[:, rows, lo:hi].rearrange("p i (c e) -> p c i e", e=2),
+                in_=(by_plane[:, rows, lo:hi] if src is None else src).rearrange("p i (c e) -> p c i e", e=2),
             )
 
         def quantise(grouped, lo, hi):
             nc.vector.quantize_mx(
                 out=codes[:, lo:hi].bitcast(FP8X4),
                 scales=scales[:, lo:hi],
-                in_=grouped[:].rearrange("p w i -> p (w i)"),
+                in_=grouped.rearrange("p w i -> p (w i)"),
             )
 
         def product(acc, m, lo, hi):
@@ -132,7 +135,7 @@ def tile_list_hboth_bias_kernel(tc, xT, w_words, w_scales, wgt, b, wgo, offs, of
         gather(0, HALF, S)
         for i in range(1, last_plane):
             gather(i, 0, S)
-        gather(last_plane, 0, LEAD)
+        gather(last_plane, 0, LEAD, lead_high[:, 0:LEAD])
         gather(last_plane, LEAD, HALF)
         gather(last_plane, HALF, S)
 
@@ -141,7 +144,9 @@ def tile_list_hboth_bias_kernel(tc, xT, w_words, w_scales, wgt, b, wgo, offs, of
         low, high, every = slice(0, 2), slice(2, PLANES), slice(0, PLANES)
         interleave(nc.scalar.copy, grouped_lead, 0, 0, LEAD, low)
         interleave(nc.scalar.copy, grouped_middle, LEAD, LEAD, LAST, low)
-        interleave(nc.scalar.copy, grouped_lead, 0, 0, LEAD, high)
+        interleave(
+            nc.scalar.copy, grouped_lead, 0, 0, LEAD, high, lead_high.rearrange("p (i c) -> p i c", i=2)[:, ::-1, :]
+        )
         interleave(nc.scalar.copy, grouped_middle, LEAD, LEAD, HALF, high)
         interleave(nc.scalar.copy, grouped_middle, LEAD, HALF, LAST, high)
         quantise(grouped_lead, 0, LEAD)
@@ -153,7 +158,7 @@ def tile_list_hboth_bias_kernel(tc, xT, w_words, w_scales, wgt, b, wgo, offs, of
             add_bias(lead[:], acc, m, 0, LEAD)
             leads.append(lead)
 
-        grouped_last = grouped_tile(S - LAST, "grouped_ends")
+        grouped_last = lead_high.bitcast(BF16).rearrange("p (w i) -> p w i", i=PLANES)
         interleave(nc.vector.tensor_copy, grouped_last, LAST, LAST, S, every)
         quantise(grouped_last, LAST, S)
         quantise(grouped_middle, LEAD, LAST)

@@ -137,7 +137,8 @@ def tile_list_hboth_bias_kernel(tc, xT, w_words, w_scales, wgt, b, wgo, offs, of
             gather(i, 0, S)
         gather(last_plane, 0, LEAD, lead_high[:, 0:LEAD])
         gather(last_plane, LEAD, HALF)
-        gather(last_plane, HALF, S)
+        gather(last_plane, HALF, LAST)
+        gather(last_plane, LAST, S)
 
         grouped_lead = grouped_tile(LEAD, "grouped_ends")
         grouped_middle = grouped_tile(LAST - LEAD, "grouped_middle")

@@ -22,6 +22,8 @@ LEAD, HALF, LAST = S // 4, S // 2, 3 * S // 4
 LEAD_TILES = 2
 EARLY_WINDOWS = 4
 PITCH = S + LEAD
+SCALE_RUNS = 4
+SCALE_COLS = M // SCALE_RUNS
 
 
 def tile_list_hboth_bias_kernel(tc, xT, w_words, w_scales, wgt, b, wgo, offs, offs2, out):
@@ -36,7 +38,7 @@ def tile_list_hboth_bias_kernel(tc, xT, w_words, w_scales, wgt, b, wgo, offs, of
         wgo_sb = keep.tile([P, S], F32, name="wgo_sb")
         planes = [keep.tile([P, T], F32, name=f"plane{i}") for i in range(PLANES)]
         w_sb = keep.tile([P, M], U32, name="w_sb", align_bytes=256)
-        ws_sb = keep.tile([P, M], U8, name="ws_sb", align_bytes=256)
+        ws_sb = keep.tile([P, SCALE_COLS], U8, name="ws_sb", align_bytes=256)
         b_rows = keep.tile([P, P], F32, name="b_rows")
         ident = keep.tile([P, P], F32, name="ident")
         b_cols = keep.tile([P, N_TILES], F32, name="b_cols")
@@ -67,7 +69,8 @@ def tile_list_hboth_bias_kernel(tc, xT, w_words, w_scales, wgt, b, wgo, offs, of
         nc.sync.dma_start(offs_out[:], offs2)
         for q in range(4):
             nc.sync.dma_start(
-                out=ws_sb[32 * q : 32 * q + 4, :].bitcast(I32), in_=w_scales[0, 4 * q : 4 * q + 4, :].bitcast(I32)
+                out=ws_sb[32 * q : 32 * q + 4 * SCALE_RUNS, :].bitcast(I32),
+                in_=w_scales[0, 4 * q : 4 * q + 4, :].bitcast(I32).rearrange("r (u c) -> u r c", u=SCALE_RUNS),
             )
         load_w(0, LEAD_TILES * P)
         nc.sync.dma_start(out=wgo_sb[:], in_=wgo)
@@ -112,10 +115,11 @@ def tile_list_hboth_bias_kernel(tc, xT, w_words, w_scales, wgt, b, wgo, offs, of
 
         def product(acc, m, lo, hi):
             cols = slice(m * P, (m + 1) * P)
+            run, first = divmod(m * P, SCALE_COLS)
             nc.tensor.matmul_mx(
                 out=acc[:, lo:hi],
                 lhsT=w_sb[:, cols].bitcast(FP8X4),
-                lhsT_scale=ws_sb[:, cols],
+                lhsT_scale=ws_sb[4 * run : P, first : first + P],
                 rhs=codes[:, lo:hi].bitcast(FP8X4),
                 rhs_scale=scales[:, lo:hi],
                 start=True,
@@ -153,10 +157,12 @@ def tile_list_hboth_bias_kernel(tc, xT, w_words, w_scales, wgt, b, wgo, offs, of
         quantise(grouped_lead, 0, LEAD)
         leads = []
         for m in range(LEAD_TILES):
-            acc = psum.tile([P, S], F32, name=f"lead_acc{m}", tag="acc")
             lead = keep.tile([P, LEAD], F32, name=f"lead{m}")
-            product(acc, m, 0, LEAD)
-            add_bias(lead[:], acc, m, 0, LEAD)
+            width = LEAD // 2 if m == 0 else LEAD
+            for lo in range(0, LEAD, width):
+                acc = psum.tile([P, S], F32, name=f"lead_acc{m}_{lo}", tag="acc")
+                product(acc, m, lo, lo + width)
+                add_bias(lead[:, lo : lo + width], acc, m, lo, lo + width)
             leads.append(lead)
 
         grouped_last = lead_high.bitcast(BF16).rearrange("p (w i) -> p w i", i=PLANES)

@@ -17,76 +17,88 @@ IDENTITY = mybir.ActivationFunctionType.Identity
 P = 128
 PLANES = 4
 GROUP = 16
+BLOCK = 32
 N_TILES = M // P
 LEAD, HALF, LAST = S // 4, S // 2, 3 * S // 4
 LEAD_TILES = 2
-EARLY_WINDOWS = 4
+WINDOWS = 3
 PITCH = S + LEAD
 SCALE_RUNS = 4
 SCALE_COLS = M // SCALE_RUNS
+ROW = 4 * T
 
 
 def tile_list_hboth_bias_kernel(tc, xT, w_words, w_scales, wgt, b, wgo, offs, offs2, out):
     nc = tc.nc
     with (
         tc.tile_pool(name="keep", bufs=1) as keep,
+        tc.tile_pool(name="shared", bufs=1) as shared,
         tc.psum_pool(name="psum", bufs=8) as psum,
     ):
         offs_in = keep.tile([P, S // GROUP], U16, name="offs_in")
         offs_out = keep.tile([P, S // GROUP], U16, name="offs_out")
-        wgt_sb = keep.tile([P, S], F32, name="wgt_sb")
-        wgo_sb = keep.tile([P, S], F32, name="wgo_sb")
-        planes = [keep.tile([P, T], F32, name=f"plane{i}") for i in range(PLANES)]
-        w_sb = keep.tile([P, M], U32, name="w_sb", align_bytes=256)
-        ws_sb = keep.tile([P, SCALE_COLS], U8, name="ws_sb", align_bytes=256)
+        wgt_sb = keep.tile([P, S], F32, name="wgt_sb", align_bytes=64)
         b_rows = keep.tile([P, P], F32, name="b_rows")
         ident = keep.tile([P, P], F32, name="ident")
         b_cols = keep.tile([P, N_TILES], F32, name="b_cols")
         picked = keep.tile([P, PLANES * PITCH], F32, name="picked", align_bytes=256)
         by_plane = picked[:].rearrange("p (i c) -> p i c", i=PLANES)
         lead_high = picked[:, 2 * PITCH - LEAD : 2 * PITCH + LEAD]
+        ws_sb = keep.tile([P, SCALE_COLS], U8, name="ws_sb", align_bytes=256)
         codes = keep.tile([P, S], U32, name="codes", align_bytes=256)
         scales = keep.tile([P, S], U8, name="scales", align_bytes=256)
 
-        def load_w(lo, hi):
-            nc.sync.dma_start(
-                out=w_sb[:, lo:hi].bitcast(I32),
-                in_=w_words[0, :, lo:hi, :].rearrange("p n t -> p (n t)").bitcast(I32),
-            )
+        def placed(name, cols, dtype, offset):
+            return shared.tile([P, cols], dtype, name=name, offset=offset, align_bytes=256)
+
+        planes = [placed(f"plane{i}", T, F32, i * ROW) for i in range(PLANES)]
+        late_windows = PLANES * ROW
+        wgt_wide = placed("wgt_wide", S, F32, late_windows + ROW - 2 * S)
+        staging = late_windows + 2 * ROW
+        wgt_pieces = placed("wgt_pieces", BLOCK, F32, staging)
+        wgt_turned = placed("wgt_turned", BLOCK, F32, staging + 512)
 
         nc.gpsimd.memset(b_rows[:], 0.0)
         nc.gpsimd.memset(ws_sb[:].bitcast(I32), 0)
         make_identity(nc, ident[:])
 
         x_view = xT.rearrange("(p i) t -> p i t", i=PLANES)
-        nc.scalar.dma_start(out=wgt_sb[:, 0:HALF], in_=wgt[:, 0:HALF])
-        nc.sync.dma_start(out=planes[0][:], in_=x_view[:, 0, :])
+        half_rows = wgt.rearrange("r (e c) -> (r e) c", e=2)[0 : 2 * P : GROUP + 1, :]
+        nc.sync.dma_start(out=wgt_pieces[:], in_=half_rows.rearrange("h (u c) -> h u c", c=BLOCK))
+        nc.scalar.dma_start(out=planes[0][:], in_=x_view[:, 0, :])
         nc.sync.dma_start(offs_in[:], offs)
-        nc.sync.dma_start(out=wgt_sb[:, HALF:S], in_=wgt[:, HALF:S])
+        nc.scalar.dma_start(out=planes[1][:], in_=x_view[:, 1, :])
         nc.sync.dma_start(out=b_rows[0:N_TILES, :], in_=b.rearrange("(m p) -> m p", p=P))
-        for i in range(1, PLANES):
-            nc.sync.dma_start(out=planes[i][:], in_=x_view[:, i, :])
+        nc.scalar.dma_start(out=planes[2][:], in_=x_view[:, 2, :])
         nc.sync.dma_start(offs_out[:], offs2)
-        for q in range(4):
-            nc.sync.dma_start(
-                out=ws_sb[32 * q : 32 * q + 4 * SCALE_RUNS, :].bitcast(I32),
-                in_=w_scales[0, 4 * q : 4 * q + 4, :].bitcast(I32).rearrange("r (u c) -> u r c", u=SCALE_RUNS),
-            )
-        load_w(0, LEAD_TILES * P)
-        nc.sync.dma_start(out=wgo_sb[:], in_=wgo)
-        load_w(LEAD_TILES * P, M)
+        nc.scalar.dma_start(out=planes[3][:], in_=x_view[:, 3, :])
 
-        windows = {}
-        for m in range(LEAD_TILES):
-            windows[m] = keep.tile([P, T], F32, name=f"window{m}")
-            nc.vector.memset(windows[m][:], 0.0)
+        windows = [keep.tile([P, T], F32, name="window0")]
+        nc.vector.memset(windows[0][:], 0.0)
 
         b_psum = psum.tile([P, S], F32, name="b_psum", tag="acc")
         nc.tensor.transpose(b_psum[:, 0:P], b_rows[:], ident[:])
         nc.scalar.activation(b_cols[:], b_psum[:, 0:N_TILES], IDENTITY)
 
-        for m, tag in enumerate(("b_rows", "ident"), start=LEAD_TILES):
-            windows[m] = keep.tile([P, T], F32, name=f"window{m}", tag=tag)
+        nc.vector.transpose(wgt_turned[:], wgt_pieces[:])
+        halves = (slice(0, HALF), slice(HALF, S))
+        turned = wgt_turned[:].rearrange("p (r u) -> p u r", r=2)
+        per_half = HALF // BLOCK
+        for h, cols in enumerate(halves):
+            nc.vector.tensor_copy(
+                out=wgt_wide[:, cols].rearrange("p (u r s) -> p u r s", r=2, s=GROUP),
+                in_=turned[:, h * per_half : (h + 1) * per_half, :].unsqueeze(3).to_broadcast([P, per_half, 2, GROUP]),
+            )
+        for cols in halves:
+            nc.vector.transpose(wgt_sb[:, cols], wgt_wide[:, cols])
+
+        for q in range(4):
+            nc.sync.dma_start(
+                out=ws_sb[32 * q : 32 * q + 4 * SCALE_RUNS, :].bitcast(I32),
+                in_=w_scales[0, 4 * q : 4 * q + 4, :].bitcast(I32).rearrange("r (u c) -> u r c", u=SCALE_RUNS),
+            )
+        for m in range(1, WINDOWS):
+            windows.append(placed(f"window{m}", T, F32, late_windows + (m - 1) * ROW))
             nc.gpsimd.memset(windows[m][:], 0.0)
 
         def gather(i, lo, hi, dst=None):
@@ -96,6 +108,30 @@ def tile_list_hboth_bias_kernel(tc, xT, w_words, w_scales, wgt, b, wgo, offs, of
                 wgt_sb[:, lo:hi],
                 MULT,
             )
+
+        last_plane = PLANES - 1
+        gather(0, 0, HALF)
+        gather(0, HALF, S)
+        for i in range(1, last_plane):
+            gather(i, 0, S)
+        gather(last_plane, 0, LEAD, lead_high[:, 0:LEAD])
+        gather(last_plane, LEAD, HALF)
+        gather(last_plane, HALF, LAST)
+        gather(last_plane, LAST, S)
+
+        lead_cols = LEAD_TILES * P
+        w_lead = placed("w_lead", lead_cols, U32, ROW)
+        wgo_sb = placed("wgo_sb", S, F32, ROW + 4 * lead_cols)
+        w_rest = placed("w_rest", M - lead_cols, U32, 2 * ROW)
+
+        def load_w(dst, lo, hi):
+            nc.sync.dma_start(
+                out=dst[:].bitcast(I32), in_=w_words[0, :, lo:hi, :].rearrange("p n t -> p (n t)").bitcast(I32)
+            )
+
+        load_w(w_lead, 0, lead_cols)
+        nc.sync.dma_start(out=wgo_sb[:], in_=wgo)
+        load_w(w_rest, lead_cols, M)
 
         def grouped_tile(width, tag):
             return keep.tile([P, width, PLANES], BF16, name=tag, tag=tag, align_bytes=256)[:]
@@ -114,11 +150,12 @@ def tile_list_hboth_bias_kernel(tc, xT, w_words, w_scales, wgt, b, wgo, offs, of
             )
 
         def product(acc, m, lo, hi):
-            cols = slice(m * P, (m + 1) * P)
-            run, first = divmod(m * P, SCALE_COLS)
+            first_col = m * P
+            words = w_lead[:, first_col : first_col + P] if m < LEAD_TILES else w_rest[:, first_col - lead_cols : first_col - lead_cols + P]
+            run, first = divmod(first_col, SCALE_COLS)
             nc.tensor.matmul_mx(
                 out=acc[:, lo:hi],
-                lhsT=w_sb[:, cols].bitcast(FP8X4),
+                lhsT=words.bitcast(FP8X4),
                 lhsT_scale=ws_sb[4 * run : P, first : first + P],
                 rhs=codes[:, lo:hi].bitcast(FP8X4),
                 rhs_scale=scales[:, lo:hi],
@@ -131,20 +168,10 @@ def tile_list_hboth_bias_kernel(tc, xT, w_words, w_scales, wgt, b, wgo, offs, of
 
         def scatter(m, y, lo, hi):
             nc.vector.tensor_tensor(
-                windows[m % EARLY_WINDOWS][:].indirect(offs_out[:, lo // GROUP : hi // GROUP]), y[:], wgo_sb[:, lo:hi], MULT
+                windows[m % WINDOWS][:].indirect(offs_out[:, lo // GROUP : hi // GROUP]), y[:], wgo_sb[:, lo:hi], MULT
             )
 
-        last_plane = PLANES - 1
-        gather(0, 0, HALF)
-        gather(0, HALF, S)
-        for i in range(1, last_plane):
-            gather(i, 0, S)
-        gather(last_plane, 0, LEAD, lead_high[:, 0:LEAD])
-        gather(last_plane, LEAD, HALF)
-        gather(last_plane, HALF, LAST)
-        gather(last_plane, LAST, S)
-
-        grouped_lead = grouped_tile(LEAD, "grouped_ends")
+        grouped_lead = grouped_tile(LEAD, "grouped_lead")
         grouped_middle = grouped_tile(LAST - LEAD, "grouped_middle")
         low, high, every = slice(0, 2), slice(2, PLANES), slice(0, PLANES)
         interleave(nc.scalar.copy, grouped_lead, 0, 0, LEAD, low)
@@ -193,4 +220,4 @@ def tile_list_hboth_bias_kernel(tc, xT, w_words, w_scales, wgt, b, wgo, offs, of
 
         for m in range(N_TILES):
             scatter(m, rests[m], LEAD if m < LEAD_TILES else 0, S)
-            nc.sync.dma_start(out=out[m * P : (m + 1) * P, :], in_=windows[m % EARLY_WINDOWS][:])
+            nc.sync.dma_start(out=out[m * P : (m + 1) * P, :], in_=windows[m % WINDOWS][:])

@@ -64,14 +64,31 @@ def tile_list_hboth_bias_kernel(tc, xT, w_words, w_scales, wgt, b, wgo, offs, of
 
         x_view = xT.rearrange("(p i) t -> p i t", i=PLANES)
         half_rows = wgt.rearrange("r (e c) -> (r e) c", e=2)[0 : 2 * P : GROUP + 1, :]
-        nc.sync.dma_start(out=wgt_pieces[:], in_=half_rows.rearrange("h (u c) -> h u c", c=BLOCK))
-        nc.scalar.dma_start(out=planes[0][:], in_=x_view[:, 0, :])
+        lead_cols = LEAD_TILES * P
+        w_lead = keep.tile([P, lead_cols], U32, name="w_lead", align_bytes=256)
+        w_rest = keep.tile([P, M - lead_cols], U32, name="w_rest", align_bytes=256)
+        wgo_sb = keep.tile([P, S], F32, name="wgo_sb")
+
+        def load_w(dst, lo, hi):
+            nc.sync.dma_start(
+                out=dst[:].bitcast(I32), in_=w_words[0, :, lo:hi, :].rearrange("p n t -> p (n t)").bitcast(I32)
+            )
+
+        nc.scalar.dma_start(out=wgt_pieces[:], in_=half_rows.rearrange("h (u c) -> h u c", c=BLOCK))
+        nc.scalar.dma_start(out=b_rows[0:N_TILES, :], in_=b.rearrange("(m p) -> m p", p=P))
+        nc.sync.dma_start(out=planes[0][:], in_=x_view[:, 0, :])
         nc.sync.dma_start(offs_in[:], offs)
-        nc.scalar.dma_start(out=planes[1][:], in_=x_view[:, 1, :])
-        nc.sync.dma_start(out=b_rows[0:N_TILES, :], in_=b.rearrange("(m p) -> m p", p=P))
-        nc.scalar.dma_start(out=planes[2][:], in_=x_view[:, 2, :])
+        for i in range(1, PLANES):
+            nc.sync.dma_start(out=planes[i][:], in_=x_view[:, i, :])
         nc.sync.dma_start(offs_out[:], offs2)
-        nc.scalar.dma_start(out=planes[3][:], in_=x_view[:, 3, :])
+        for q in range(4):
+            nc.sync.dma_start(
+                out=ws_sb[32 * q : 32 * q + 4 * SCALE_RUNS, :].bitcast(I32),
+                in_=w_scales[0, 4 * q : 4 * q + 4, :].bitcast(I32).rearrange("r (u c) -> u r c", u=SCALE_RUNS),
+            )
+        load_w(w_lead, 0, lead_cols)
+        nc.sync.dma_start(out=wgo_sb[:], in_=wgo)
+        load_w(w_rest, lead_cols, M)
 
         windows = [keep.tile([P, T], F32, name="window0")]
         nc.vector.memset(windows[0][:], 0.0)
@@ -92,11 +109,6 @@ def tile_list_hboth_bias_kernel(tc, xT, w_words, w_scales, wgt, b, wgo, offs, of
         for cols in halves:
             nc.vector.transpose(wgt_sb[:, cols], wgt_wide[:, cols])
 
-        for q in range(4):
-            nc.sync.dma_start(
-                out=ws_sb[32 * q : 32 * q + 4 * SCALE_RUNS, :].bitcast(I32),
-                in_=w_scales[0, 4 * q : 4 * q + 4, :].bitcast(I32).rearrange("r (u c) -> u r c", u=SCALE_RUNS),
-            )
         for m in range(1, WINDOWS):
             windows.append(placed(f"window{m}", T, F32, late_windows + (m - 1) * ROW))
             nc.gpsimd.memset(windows[m][:], 0.0)
@@ -118,20 +130,6 @@ def tile_list_hboth_bias_kernel(tc, xT, w_words, w_scales, wgt, b, wgo, offs, of
         gather(last_plane, LEAD, HALF)
         gather(last_plane, HALF, LAST)
         gather(last_plane, LAST, S)
-
-        lead_cols = LEAD_TILES * P
-        w_lead = placed("w_lead", lead_cols, U32, ROW)
-        wgo_sb = placed("wgo_sb", S, F32, ROW + 4 * lead_cols)
-        w_rest = placed("w_rest", M - lead_cols, U32, 2 * ROW)
-
-        def load_w(dst, lo, hi):
-            nc.sync.dma_start(
-                out=dst[:].bitcast(I32), in_=w_words[0, :, lo:hi, :].rearrange("p n t -> p (n t)").bitcast(I32)
-            )
-
-        load_w(w_lead, 0, lead_cols)
-        nc.sync.dma_start(out=wgo_sb[:], in_=wgo)
-        load_w(w_rest, lead_cols, M)
 
         def grouped_tile(width, tag):
             return keep.tile([P, width, PLANES], BF16, name=tag, tag=tag, align_bytes=256)[:]

@@ -22,7 +22,8 @@ N_TILES = M // P
 LEAD, HALF, LAST = S // 4, S // 2, 3 * S // 4
 LEAD_TILES = 2
 WINDOWS = 3
-PITCH = S + LEAD
+LOW_AT, WGT_AT, ENDS_AT, THIRD_AT = 0, 2 * S + LAST, 3 * S + LAST, 4 * S
+FOURTH_AT = THIRD_AT + LAST - LEAD
 SCALE_RUNS = 4
 SCALE_COLS = M // SCALE_RUNS
 ROW = 4 * T
@@ -37,13 +38,16 @@ def tile_list_hboth_bias_kernel(tc, xT, w_words, w_scales, wgt, b, wgo, offs, of
     ):
         offs_in = keep.tile([P, S // GROUP], U16, name="offs_in")
         offs_out = keep.tile([P, S // GROUP], U16, name="offs_out")
-        wgt_sb = keep.tile([P, S], F32, name="wgt_sb", align_bytes=64)
         b_rows = keep.tile([P, P], F32, name="b_rows")
         ident = keep.tile([P, P], F32, name="ident")
         b_cols = keep.tile([P, N_TILES], F32, name="b_cols")
-        picked = keep.tile([P, PLANES * PITCH], F32, name="picked", align_bytes=256)
-        by_plane = picked[:].rearrange("p (i c) -> p i c", i=PLANES)
-        lead_high = picked[:, 2 * PITCH - LEAD : 2 * PITCH + LEAD]
+        work = keep.tile([P, 2 * FOURTH_AT], F32, name="work", align_bytes=256)
+        wgt_sb = work[:, WGT_AT : WGT_AT + S]
+
+        def pair(first, second, width):
+            step = second - first
+            return work[:, first : first + 2 * step].rearrange("p (i c) -> p i c", i=2)[:, :, 0:width]
+
         ws_sb = keep.tile([P, SCALE_COLS], U8, name="ws_sb", align_bytes=256)
         codes = keep.tile([P, S], U32, name="codes", align_bytes=256)
         scales = keep.tile([P, S], U8, name="scales", align_bytes=256)
@@ -74,13 +78,13 @@ def tile_list_hboth_bias_kernel(tc, xT, w_words, w_scales, wgt, b, wgo, offs, of
                 out=dst[:].bitcast(I32), in_=w_words[0, :, lo:hi, :].rearrange("p n t -> p (n t)").bitcast(I32)
             )
 
-        nc.scalar.dma_start(out=wgt_pieces[:], in_=half_rows.rearrange("h (u c) -> h u c", c=BLOCK))
-        nc.scalar.dma_start(out=b_rows[0:N_TILES, :], in_=b.rearrange("(m p) -> m p", p=P))
-        nc.sync.dma_start(out=planes[0][:], in_=x_view[:, 0, :])
+        nc.sync.dma_start(out=wgt_pieces[:], in_=half_rows.rearrange("h (u c) -> h u c", c=BLOCK))
+        nc.scalar.dma_start(out=planes[0][:], in_=x_view[:, 0, :])
         nc.sync.dma_start(offs_in[:], offs)
+        nc.sync.dma_start(offs_out[:], offs2)
+        nc.sync.dma_start(out=b_rows[0:N_TILES, :], in_=b.rearrange("(m p) -> m p", p=P))
         for i in range(1, PLANES):
             nc.sync.dma_start(out=planes[i][:], in_=x_view[:, i, :])
-        nc.sync.dma_start(offs_out[:], offs2)
         for q in range(4):
             nc.sync.dma_start(
                 out=ws_sb[32 * q : 32 * q + 4 * SCALE_RUNS, :].bitcast(I32),
@@ -113,31 +117,29 @@ def tile_list_hboth_bias_kernel(tc, xT, w_words, w_scales, wgt, b, wgo, offs, of
             windows.append(placed(f"window{m}", T, F32, late_windows + (m - 1) * ROW))
             nc.gpsimd.memset(windows[m][:], 0.0)
 
-        def gather(i, lo, hi, dst=None):
+        def gather(i, lo, hi, at):
             nc.vector.tensor_tensor(
-                picked[:, i * PITCH + lo : i * PITCH + hi] if dst is None else dst,
+                work[:, at : at + hi - lo],
                 planes[i][:].indirect(offs_in[:, lo // GROUP : hi // GROUP]),
                 wgt_sb[:, lo:hi],
                 MULT,
             )
 
-        last_plane = PLANES - 1
-        gather(0, 0, HALF)
-        gather(0, HALF, S)
-        for i in range(1, last_plane):
-            gather(i, 0, S)
-        gather(last_plane, 0, LEAD, lead_high[:, 0:LEAD])
-        gather(last_plane, LEAD, HALF)
-        gather(last_plane, HALF, LAST)
-        gather(last_plane, LAST, S)
+        gather(0, 0, HALF, LOW_AT)
+        gather(0, HALF, S, LOW_AT + HALF)
+        gather(1, 0, S, LOW_AT + S)
+        gather(2, 0, LAST, THIRD_AT)
+        gather(3, 0, LEAD, ENDS_AT)
+        gather(3, LEAD, HALF, FOURTH_AT + LEAD)
+        gather(2, LAST, S, WGT_AT)
+        gather(3, HALF, LAST, FOURTH_AT + HALF)
 
         def grouped_tile(width, tag):
             return keep.tile([P, width, PLANES], BF16, name=tag, tag=tag, align_bytes=256)[:]
 
-        def interleave(engine_copy, grouped, first, lo, hi, rows, src=None):
+        def interleave(engine_copy, grouped, src):
             engine_copy(
-                out=grouped[:, lo - first : hi - first, rows].rearrange("p (c e) i -> p c i e", e=2),
-                in_=(by_plane[:, rows, lo:hi] if src is None else src).rearrange("p i (c e) -> p c i e", e=2),
+                out=grouped.rearrange("p (c e) i -> p c i e", e=2), in_=src.rearrange("p i (c e) -> p c i e", e=2)
             )
 
         def quantise(grouped, lo, hi):
@@ -171,15 +173,17 @@ def tile_list_hboth_bias_kernel(tc, xT, w_words, w_scales, wgt, b, wgo, offs, of
 
         grouped_lead = grouped_tile(LEAD, "grouped_lead")
         grouped_middle = grouped_tile(LAST - LEAD, "grouped_middle")
-        low, high, every = slice(0, 2), slice(2, PLANES), slice(0, PLANES)
-        interleave(nc.scalar.copy, grouped_lead, 0, 0, LEAD, low)
-        interleave(nc.scalar.copy, grouped_middle, LEAD, LEAD, LAST, low)
-        interleave(
-            nc.scalar.copy, grouped_lead, 0, 0, LEAD, high, lead_high.rearrange("p (i c) -> p i c", i=2)[:, ::-1, :]
-        )
-        interleave(nc.scalar.copy, grouped_middle, LEAD, LEAD, HALF, high)
-        interleave(nc.scalar.copy, grouped_middle, LEAD, HALF, LAST, high)
+        grouped_last = grouped_tile(S - LAST, "grouped_last")
+        low, high = slice(0, 2), slice(2, PLANES)
+        interleave(nc.scalar.copy, grouped_lead[:, :, low], pair(LOW_AT, LOW_AT + S, LEAD))
+        interleave(nc.scalar.copy, grouped_middle[:, :, low], pair(LOW_AT + LEAD, LOW_AT + S + LEAD, LAST - LEAD))
+        interleave(nc.scalar.copy, grouped_lead[:, :, high], pair(ENDS_AT, THIRD_AT, LEAD)[:, ::-1, :])
+        for lo in (LEAD, HALF):
+            interleave(
+                nc.scalar.copy, grouped_middle[:, lo - LEAD : lo, high], pair(THIRD_AT + lo, FOURTH_AT + lo, LEAD)
+            )
         quantise(grouped_lead, 0, LEAD)
+        gather(3, LAST, S, ENDS_AT)
         leads = []
         for m in range(LEAD_TILES):
             lead = keep.tile([P, LEAD], F32, name=f"lead{m}")
@@ -190,10 +194,11 @@ def tile_list_hboth_bias_kernel(tc, xT, w_words, w_scales, wgt, b, wgo, offs, of
                 add_bias(lead[:, lo : lo + width], acc, m, lo, lo + width)
             leads.append(lead)
 
-        grouped_last = lead_high.bitcast(BF16).rearrange("p (w i) -> p w i", i=PLANES)
-        interleave(nc.vector.tensor_copy, grouped_last, LAST, LAST, S, every)
+        quantise(grouped_middle[:, 0:LEAD, :], LEAD, HALF)
+        last_quarters = work[:, LAST : LAST + PLANES * S].rearrange("p (i c) -> p i c", i=PLANES)[:, :, 0:LEAD]
+        interleave(nc.vector.tensor_copy, grouped_last, last_quarters)
+        quantise(grouped_middle[:, LEAD:HALF, :], HALF, LAST)
         quantise(grouped_last, LAST, S)
-        quantise(grouped_middle, LEAD, LAST)
         for m in range(LEAD_TILES):
             scatter(m, leads[m], 0, LEAD)
 
@@ -202,15 +207,15 @@ def tile_list_hboth_bias_kernel(tc, xT, w_words, w_scales, wgt, b, wgo, offs, of
             lo = LEAD if m < LEAD_TILES else 0
             rest = keep.tile([P, S - lo], F32, name=f"rest{m}", tag=f"rest{m}")
             if m == 0:
-                for part_lo, part_hi in ((LAST, S), (LEAD, LAST)):
+                for part_lo, part_hi in ((LEAD, LAST), (LAST, S)):
                     part_acc = psum.tile([P, S], F32, name=f"part_acc{part_lo}", tag="acc")
                     product(part_acc, m, part_lo, part_hi)
                     add_bias(rest[:, part_lo - lo : part_hi - lo], part_acc, m, part_lo, part_hi)
             else:
                 acc = psum.tile([P, S], F32, name=f"acc{m}", tag="acc")
                 if m < LEAD_TILES:
-                    product(acc, m, LAST, S)
                     product(acc, m, LEAD, LAST)
+                    product(acc, m, LAST, S)
                 else:
                     product(acc, m, 0, S)
                 add_bias(rest[:], acc, m, lo, S)

@@ -223,4 +223,5 @@ def tile_list_hboth_bias_kernel(tc, xT, w_words, w_scales, wgt, b, wgo, offs, of
 
         for m in range(N_TILES):
             scatter(m, rests[m], LEAD if m < LEAD_TILES else 0, S)
-            nc.sync.dma_start(out=out[m * P : (m + 1) * P, :], in_=windows[m % WINDOWS][:])
+            queue = nc.scalar if m == N_TILES - 1 else nc.sync
+            queue.dma_start(out=out[m * P : (m + 1) * P, :], in_=windows[m % WINDOWS][:])

@@ -50,12 +50,17 @@ def tile_list_hboth_bias_kernel(tc, xT, w_words, w_scales, wgt, b, wgo, offs, of
 
         ws_sb = keep.tile([P, SCALE_COLS], U8, name="ws_sb", align_bytes=256)
         codes = keep.tile([P, S], U32, name="codes", align_bytes=256)
-        scales = keep.tile([P, S], U8, name="scales", align_bytes=256)
 
         def placed(name, cols, dtype, offset):
             return shared.tile([P, cols], dtype, name=name, offset=offset, align_bytes=256)
 
         planes = [placed(f"plane{i}", T, F32, i * ROW) for i in range(PLANES)]
+        early_scales = keep.tile([P, HALF], U8, name="early_scales", align_bytes=256)
+        late_scales = placed("late_scales", HALF, U8, (PLANES - 1) * ROW)
+
+        def scales(lo, hi):
+            return early_scales[:, lo:hi] if hi <= HALF else late_scales[:, lo - HALF : hi - HALF]
+
         late_windows = PLANES * ROW
         wgt_wide = placed("wgt_wide", S, F32, late_windows + ROW - 2 * S)
         staging = late_windows + 2 * ROW
@@ -81,7 +86,6 @@ def tile_list_hboth_bias_kernel(tc, xT, w_words, w_scales, wgt, b, wgo, offs, of
         nc.sync.dma_start(out=wgt_pieces[:], in_=half_rows.rearrange("h (u c) -> h u c", c=BLOCK))
         nc.scalar.dma_start(out=planes[0][:], in_=x_view[:, 0, :])
         nc.sync.dma_start(offs_in[:], offs)
-        nc.sync.dma_start(offs_out[:], offs2)
         nc.sync.dma_start(out=b_rows[0:N_TILES, :], in_=b.rearrange("(m p) -> m p", p=P))
         for i in range(1, PLANES):
             nc.sync.dma_start(out=planes[i][:], in_=x_view[:, i, :])
@@ -91,6 +95,7 @@ def tile_list_hboth_bias_kernel(tc, xT, w_words, w_scales, wgt, b, wgo, offs, of
                 in_=w_scales[0, 4 * q : 4 * q + 4, :].bitcast(I32).rearrange("r (u c) -> u r c", u=SCALE_RUNS),
             )
         load_w(w_lead, 0, lead_cols)
+        nc.sync.dma_start(offs_out[:], offs2)
         nc.sync.dma_start(out=wgo_sb[:], in_=wgo)
         load_w(w_rest, lead_cols, M)
 
@@ -145,7 +150,7 @@ def tile_list_hboth_bias_kernel(tc, xT, w_words, w_scales, wgt, b, wgo, offs, of
         def quantise(grouped, lo, hi):
             nc.vector.quantize_mx(
                 out=codes[:, lo:hi].bitcast(FP8X4),
-                scales=scales[:, lo:hi],
+                scales=scales(lo, hi),
                 in_=grouped.rearrange("p w i -> p (w i)"),
             )
 
@@ -153,15 +158,16 @@ def tile_list_hboth_bias_kernel(tc, xT, w_words, w_scales, wgt, b, wgo, offs, of
             first_col = m * P
             words = w_lead[:, first_col : first_col + P] if m < LEAD_TILES else w_rest[:, first_col - lead_cols : first_col - lead_cols + P]
             run, first = divmod(first_col, SCALE_COLS)
-            nc.tensor.matmul_mx(
-                out=acc[:, lo:hi],
-                lhsT=words.bitcast(FP8X4),
-                lhsT_scale=ws_sb[4 * run : P, first : first + P],
-                rhs=codes[:, lo:hi].bitcast(FP8X4),
-                rhs_scale=scales[:, lo:hi],
-                start=True,
-                stop=True,
-            )
+            for part_lo, part_hi in ((lo, HALF), (HALF, hi)) if lo < HALF < hi else ((lo, hi),):
+                nc.tensor.matmul_mx(
+                    out=acc[:, part_lo:part_hi],
+                    lhsT=words.bitcast(FP8X4),
+                    lhsT_scale=ws_sb[4 * run : P, first : first + P],
+                    rhs=codes[:, part_lo:part_hi].bitcast(FP8X4),
+                    rhs_scale=scales(part_lo, part_hi),
+                    start=True,
+                    stop=True,
+                )
 
         def add_bias(y, acc, m, lo, hi):
             nc.scalar.activation(y, acc[:, lo:hi], IDENTITY, bias=b_cols[:, m : m + 1])

@@ -229,5 +229,7 @@ def tile_list_hboth_bias_kernel(tc, xT, w_words, w_scales, wgt, b, wgo, offs, of
 
         for m in range(N_TILES):
             scatter(m, rests[m], LEAD if m < LEAD_TILES else 0, S)
-            queue = nc.scalar if m == N_TILES - 1 else nc.sync
-            queue.dma_start(out=out[m * P : (m + 1) * P, :], in_=windows[m % WINDOWS][:])
+            if m == N_TILES - 1:
+                nc.scalar.dma_start(out=out[m * P : (m + 1) * P, :], in_=windows[m % WINDOWS][:], max_dma_last_dim=1024)
+            else:
+                nc.sync.dma_start(out=out[m * P : (m + 1) * P, :], in_=windows[m % WINDOWS][:])

@@ -22,8 +22,10 @@ N_TILES = M // P
 LEAD, HALF, LAST = S // 4, S // 2, 3 * S // 4
 LEAD_TILES = 2
 WINDOWS = 3
-LOW_AT, WGT_AT, ENDS_AT, THIRD_AT = 0, 2 * S + LAST, 3 * S + LAST, 4 * S
-FOURTH_AT = THIRD_AT + LAST - LEAD
+WGT_AT, ENDS_AT, THIRD_AT = 0, S, S + LEAD
+FOURTH_AT = THIRD_AT + S
+LOW_AT = FOURTH_AT + S
+BYTE_OF = (2, 3, 0, 1)
 SCALE_RUNS = 4
 SCALE_COLS = M // SCALE_RUNS
 ROW = 4 * T
@@ -41,12 +43,17 @@ def tile_list_hboth_bias_kernel(tc, xT, w_words, w_scales, wgt, b, wgo, offs, of
         b_rows = keep.tile([P, P], F32, name="b_rows")
         ident = keep.tile([P, P], F32, name="ident")
         b_cols = keep.tile([P, N_TILES], F32, name="b_cols")
-        work = keep.tile([P, 2 * FOURTH_AT], F32, name="work", align_bytes=256)
+        work = keep.tile([P, 8 * S], F32, name="work", align_bytes=256)
         wgt_sb = work[:, WGT_AT : WGT_AT + S]
 
         def pair(first, second, width):
             step = second - first
             return work[:, first : first + 2 * step].rearrange("p (i c) -> p i c", i=2)[:, :, 0:width]
+
+        def four(high_at, low_at):
+            step = low_at - high_at
+            both = work[:, high_at : high_at + 2 * step].rearrange("p (h i c) -> p h i c", h=2, c=S)
+            return both[:, :, 0:2, 0:LEAD]
 
         ws_sb = keep.tile([P, SCALE_COLS], U8, name="ws_sb", align_bytes=256)
         codes = keep.tile([P, S], U32, name="codes", align_bytes=256)
@@ -84,11 +91,11 @@ def tile_list_hboth_bias_kernel(tc, xT, w_words, w_scales, wgt, b, wgo, offs, of
             )
 
         nc.sync.dma_start(out=wgt_pieces[:], in_=half_rows.rearrange("h (u c) -> h u c", c=BLOCK))
-        nc.scalar.dma_start(out=planes[0][:], in_=x_view[:, 0, :])
+        nc.scalar.dma_start(out=planes[0][:], in_=x_view[:, BYTE_OF[0], :])
         nc.sync.dma_start(offs_in[:], offs)
         nc.sync.dma_start(out=b_rows[0:N_TILES, :], in_=b.rearrange("(m p) -> m p", p=P))
         for i in range(1, PLANES):
-            nc.sync.dma_start(out=planes[i][:], in_=x_view[:, i, :])
+            nc.sync.dma_start(out=planes[i][:], in_=x_view[:, BYTE_OF[i], :])
         for q in range(4):
             nc.sync.dma_start(
                 out=ws_sb[32 * q : 32 * q + 4 * SCALE_RUNS, :].bitcast(I32),
@@ -147,6 +154,12 @@ def tile_list_hboth_bias_kernel(tc, xT, w_words, w_scales, wgt, b, wgo, offs, of
                 out=grouped.rearrange("p (c e) i -> p c i e", e=2), in_=src.rearrange("p i (c e) -> p c i e", e=2)
             )
 
+        def interleave_whole(engine_copy, grouped, src):
+            engine_copy(
+                out=grouped.rearrange("p (c e) (h i) -> p c h i e", e=2, h=2),
+                in_=src.rearrange("p h i (c e) -> p c h i e", e=2),
+            )
+
         def quantise(grouped, lo, hi):
             nc.vector.quantize_mx(
                 out=codes[:, lo:hi].bitcast(FP8X4),
@@ -177,17 +190,15 @@ def tile_list_hboth_bias_kernel(tc, xT, w_words, w_scales, wgt, b, wgo, offs, of
                 windows[m % WINDOWS][:].indirect(offs_out[:, lo // GROUP : hi // GROUP]), y[:], wgo_sb[:, lo:hi], MULT
             )
 
-        grouped_lead = grouped_tile(LEAD, "grouped_lead")
-        grouped_middle = grouped_tile(LAST - LEAD, "grouped_middle")
+        grouped_front = grouped_tile(HALF, "grouped_front")
+        grouped_lead, grouped_second = grouped_front[:, 0:LEAD, :], grouped_front[:, LEAD:HALF, :]
+        grouped_third = grouped_tile(LAST - HALF, "grouped_third")
         grouped_last = grouped_tile(S - LAST, "grouped_last")
-        low, high = slice(0, 2), slice(2, PLANES)
-        interleave(nc.scalar.copy, grouped_lead[:, :, low], pair(LOW_AT, LOW_AT + S, LEAD))
-        interleave(nc.scalar.copy, grouped_middle[:, :, low], pair(LOW_AT + LEAD, LOW_AT + S + LEAD, LAST - LEAD))
+        low, high = slice(2, PLANES), slice(0, 2)
+        interleave(nc.scalar.copy, grouped_front[:, :, low], pair(LOW_AT, LOW_AT + S, HALF))
         interleave(nc.scalar.copy, grouped_lead[:, :, high], pair(ENDS_AT, THIRD_AT, LEAD)[:, ::-1, :])
-        for lo in (LEAD, HALF):
-            interleave(
-                nc.scalar.copy, grouped_middle[:, lo - LEAD : lo, high], pair(THIRD_AT + lo, FOURTH_AT + lo, LEAD)
-            )
+        interleave(nc.scalar.copy, grouped_second[:, :, high], pair(THIRD_AT + LEAD, FOURTH_AT + LEAD, LEAD))
+        interleave_whole(nc.scalar.copy, grouped_third, four(THIRD_AT + HALF, LOW_AT + HALF))
         quantise(grouped_lead, 0, LEAD)
         gather(3, LAST, S, ENDS_AT)
         leads = []
@@ -200,10 +211,9 @@ def tile_list_hboth_bias_kernel(tc, xT, w_words, w_scales, wgt, b, wgo, offs, of
                 add_bias(lead[:, lo : lo + width], acc, m, lo, lo + width)
             leads.append(lead)
 
-        quantise(grouped_middle[:, 0:LEAD, :], LEAD, HALF)
-        last_quarters = work[:, LAST : LAST + PLANES * S].rearrange("p (i c) -> p i c", i=PLANES)[:, :, 0:LEAD]
-        interleave(nc.vector.tensor_copy, grouped_last, last_quarters)
-        quantise(grouped_middle[:, LEAD:HALF, :], HALF, LAST)
+        quantise(grouped_second, LEAD, HALF)
+        interleave_whole(nc.vector.tensor_copy, grouped_last, four(WGT_AT, LOW_AT + LAST))
+        quantise(grouped_third, HALF, LAST)
         quantise(grouped_last, LAST, S)
         for m in range(LEAD_TILES):
             scatter(m, leads[m], 0, LEAD)

@@ -43,7 +43,7 @@ def tile_list_hboth_bias_kernel(tc, xT, w_words, w_scales, wgt, b, wgo, offs, of
         b_rows = keep.tile([P, P], F32, name="b_rows")
         ident = keep.tile([P, P], F32, name="ident")
         b_cols = keep.tile([P, N_TILES], F32, name="b_cols")
-        work = keep.tile([P, 8 * S], F32, name="work", align_bytes=256)
+        work = keep.tile([P, 9 * S], F32, name="work", align_bytes=256)
         wgt_sb = work[:, WGT_AT : WGT_AT + S]
 
         def pair(first, second, width):

import concourse.mybir as mybir
from concourse.masks import make_identity

K, M, T, S = 512, 1024, 1024, 512
FLOPS = 2 * K * M * S

F32 = mybir.dt.float32
BF16 = mybir.dt.bfloat16
I32 = mybir.dt.int32
U32 = mybir.dt.uint32
U16 = mybir.dt.uint16
U8 = mybir.dt.uint8
FP8X4 = mybir.dt.float8_e4m3fn_x4
MULT = mybir.AluOpType.mult
IDENTITY = mybir.ActivationFunctionType.Identity

P = 128
PLANES = 4
GROUP = 16
BLOCK = 32
N_TILES = M // P
LEAD, HALF, LAST = S // 4, S // 2, 3 * S // 4
LEAD_TILES = 2
WINDOWS = 3
WGT_AT, ENDS_AT, THIRD_AT = 0, S, S + LEAD
FOURTH_AT = THIRD_AT + S
LOW_AT = FOURTH_AT + S
BYTE_OF = (2, 3, 0, 1)
SCALE_RUNS = 4
SCALE_COLS = M // SCALE_RUNS
ROW = 4 * T


def tile_list_hboth_bias_kernel(tc, xT, w_words, w_scales, wgt, b, wgo, offs, offs2, out):
    nc = tc.nc
    with (
        tc.tile_pool(name="keep", bufs=1) as keep,
        tc.tile_pool(name="shared", bufs=1) as shared,
        tc.psum_pool(name="psum", bufs=8) as psum,
    ):
        offs_in = keep.tile([P, S // GROUP], U16, name="offs_in")
        offs_out = keep.tile([P, S // GROUP], U16, name="offs_out")
        b_rows = keep.tile([P, P], F32, name="b_rows")
        ident = keep.tile([P, P], F32, name="ident")
        b_cols = keep.tile([P, N_TILES], F32, name="b_cols")
        work = keep.tile([P, 9 * S], F32, name="work", align_bytes=256)
        wgt_sb = work[:, WGT_AT : WGT_AT + S]

        def pair(first, second, width):
            step = second - first
            return work[:, first : first + 2 * step].rearrange("p (i c) -> p i c", i=2)[:, :, 0:width]

        def four(high_at, low_at):
            step = low_at - high_at
            both = work[:, high_at : high_at + 2 * step].rearrange("p (h i c) -> p h i c", h=2, c=S)
            return both[:, :, 0:2, 0:LEAD]

        ws_sb = keep.tile([P, SCALE_COLS], U8, name="ws_sb", align_bytes=256)
        codes = keep.tile([P, S], U32, name="codes", align_bytes=256)

        def placed(name, cols, dtype, offset):
            return shared.tile([P, cols], dtype, name=name, offset=offset, align_bytes=256)

        planes = [placed(f"plane{i}", T, F32, i * ROW) for i in range(PLANES)]
        early_scales = keep.tile([P, HALF], U8, name="early_scales", align_bytes=256)
        late_scales = placed("late_scales", HALF, U8, (PLANES - 1) * ROW)

        def scales(lo, hi):
            return early_scales[:, lo:hi] if hi <= HALF else late_scales[:, lo - HALF : hi - HALF]

        late_windows = PLANES * ROW
        wgt_wide = placed("wgt_wide", S, F32, late_windows + ROW - 2 * S)
        staging = late_windows + 2 * ROW
        wgt_pieces = placed("wgt_pieces", BLOCK, F32, staging)
        wgt_turned = placed("wgt_turned", BLOCK, F32, staging + 512)

        nc.gpsimd.memset(b_rows[:], 0.0)
        nc.gpsimd.memset(ws_sb[:].bitcast(I32), 0)
        make_identity(nc, ident[:])

        x_view = xT.rearrange("(p i) t -> p i t", i=PLANES)
        half_rows = wgt.rearrange("r (e c) -> (r e) c", e=2)[0 : 2 * P : GROUP + 1, :]
        lead_cols = LEAD_TILES * P
        w_lead = keep.tile([P, lead_cols], U32, name="w_lead", align_bytes=256)
        w_rest = keep.tile([P, M - lead_cols], U32, name="w_rest", align_bytes=256)
        wgo_sb = keep.tile([P, S], F32, name="wgo_sb")

        def load_w(dst, lo, hi):
            nc.sync.dma_start(
                out=dst[:].bitcast(I32), in_=w_words[0, :, lo:hi, :].rearrange("p n t -> p (n t)").bitcast(I32)
            )

        nc.sync.dma_start(out=wgt_pieces[:], in_=half_rows.rearrange("h (u c) -> h u c", c=BLOCK))
        nc.scalar.dma_start(out=planes[0][:], in_=x_view[:, BYTE_OF[0], :])
        nc.sync.dma_start(offs_in[:], offs)
        nc.sync.dma_start(out=b_rows[0:N_TILES, :], in_=b.rearrange("(m p) -> m p", p=P))
        for i in range(1, PLANES):
            nc.sync.dma_start(out=planes[i][:], in_=x_view[:, BYTE_OF[i], :])
        for q in range(4):
            nc.sync.dma_start(
                out=ws_sb[32 * q : 32 * q + 4 * SCALE_RUNS, :].bitcast(I32),
                in_=w_scales[0, 4 * q : 4 * q + 4, :].bitcast(I32).rearrange("r (u c) -> u r c", u=SCALE_RUNS),
            )
        load_w(w_lead, 0, lead_cols)
        nc.sync.dma_start(offs_out[:], offs2)
        nc.sync.dma_start(out=wgo_sb[:], in_=wgo)
        load_w(w_rest, lead_cols, M)

        windows = [keep.tile([P, T], F32, name="window0")]
        nc.vector.memset(windows[0][:], 0.0)

        b_psum = psum.tile([P, S], F32, name="b_psum", tag="acc")
        nc.tensor.transpose(b_psum[:, 0:P], b_rows[:], ident[:])
        nc.scalar.activation(b_cols[:], b_psum[:, 0:N_TILES], IDENTITY)

        nc.vector.transpose(wgt_turned[:], wgt_pieces[:])
        halves = (slice(0, HALF), slice(HALF, S))
        turned = wgt_turned[:].rearrange("p (r u) -> p u r", r=2)
        per_half = HALF // BLOCK
        for h, cols in enumerate(halves):
            nc.vector.tensor_copy(
                out=wgt_wide[:, cols].rearrange("p (u r s) -> p u r s", r=2, s=GROUP),
                in_=turned[:, h * per_half : (h + 1) * per_half, :].unsqueeze(3).to_broadcast([P, per_half, 2, GROUP]),
            )
        for cols in halves:
            nc.vector.transpose(wgt_sb[:, cols], wgt_wide[:, cols])

        for m in range(1, WINDOWS):
            windows.append(placed(f"window{m}", T, F32, late_windows + (m - 1) * ROW))
            nc.gpsimd.memset(windows[m][:], 0.0)

        def gather(i, lo, hi, at):
            nc.vector.tensor_tensor(
                work[:, at : at + hi - lo],
                planes[i][:].indirect(offs_in[:, lo // GROUP : hi // GROUP]),
                wgt_sb[:, lo:hi],
                MULT,
            )

        gather(0, 0, HALF, LOW_AT)
        gather(0, HALF, S, LOW_AT + HALF)
        gather(1, 0, S, LOW_AT + S)
        gather(2, 0, LAST, THIRD_AT)
        gather(3, 0, LEAD, ENDS_AT)
        gather(3, LEAD, HALF, FOURTH_AT + LEAD)
        gather(2, LAST, S, WGT_AT)
        gather(3, HALF, LAST, FOURTH_AT + HALF)

        def grouped_tile(width, tag):
            return keep.tile([P, width, PLANES], BF16, name=tag, tag=tag, align_bytes=256)[:]

        def interleave(engine_copy, grouped, src):
            engine_copy(
                out=grouped.rearrange("p (c e) i -> p c i e", e=2), in_=src.rearrange("p i (c e) -> p c i e", e=2)
            )

        def interleave_whole(engine_copy, grouped, src):
            engine_copy(
                out=grouped.rearrange("p (c e) (h i) -> p c h i e", e=2, h=2),
                in_=src.rearrange("p h i (c e) -> p c h i e", e=2),
            )

        def quantise(grouped, lo, hi):
            nc.vector.quantize_mx(
                out=codes[:, lo:hi].bitcast(FP8X4),
                scales=scales(lo, hi),
                in_=grouped.rearrange("p w i -> p (w i)"),
            )

        def product(acc, m, lo, hi):
            first_col = m * P
            words = w_lead[:, first_col : first_col + P] if m < LEAD_TILES else w_rest[:, first_col - lead_cols : first_col - lead_cols + P]
            run, first = divmod(first_col, SCALE_COLS)
            for part_lo, part_hi in ((lo, HALF), (HALF, hi)) if lo < HALF < hi else ((lo, hi),):
                nc.tensor.matmul_mx(
                    out=acc[:, part_lo:part_hi],
                    lhsT=words.bitcast(FP8X4),
                    lhsT_scale=ws_sb[4 * run : P, first : first + P],
                    rhs=codes[:, part_lo:part_hi].bitcast(FP8X4),
                    rhs_scale=scales(part_lo, part_hi),
                    start=True,
                    stop=True,
                )

        def add_bias(y, acc, m, lo, hi):
            nc.scalar.activation(y, acc[:, lo:hi], IDENTITY, bias=b_cols[:, m : m + 1])

        def scatter(m, y, lo, hi):
            nc.vector.tensor_tensor(
                windows[m % WINDOWS][:].indirect(offs_out[:, lo // GROUP : hi // GROUP]), y[:], wgo_sb[:, lo:hi], MULT
            )

        grouped_front = grouped_tile(HALF, "grouped_front")
        grouped_lead, grouped_second = grouped_front[:, 0:LEAD, :], grouped_front[:, LEAD:HALF, :]
        grouped_third = grouped_tile(LAST - HALF, "grouped_third")
        grouped_last = grouped_tile(S - LAST, "grouped_last")
        low, high = slice(2, PLANES), slice(0, 2)
        interleave(nc.scalar.copy, grouped_front[:, :, low], pair(LOW_AT, LOW_AT + S, HALF))
        interleave(nc.scalar.copy, grouped_lead[:, :, high], pair(ENDS_AT, THIRD_AT, LEAD)[:, ::-1, :])
        interleave(nc.scalar.copy, grouped_second[:, :, high], pair(THIRD_AT + LEAD, FOURTH_AT + LEAD, LEAD))
        interleave_whole(nc.scalar.copy, grouped_third, four(THIRD_AT + HALF, LOW_AT + HALF))
        quantise(grouped_lead, 0, LEAD)
        gather(3, LAST, S, ENDS_AT)
        leads = []
        for m in range(LEAD_TILES):
            lead = keep.tile([P, LEAD], F32, name=f"lead{m}")
            width = LEAD // 2 if m == 0 else LEAD
            for lo in range(0, LEAD, width):
                acc = psum.tile([P, S], F32, name=f"lead_acc{m}_{lo}", tag="acc")
                product(acc, m, lo, lo + width)
                add_bias(lead[:, lo : lo + width], acc, m, lo, lo + width)
            leads.append(lead)

        quantise(grouped_second, LEAD, HALF)
        interleave_whole(nc.vector.tensor_copy, grouped_last, four(WGT_AT, LOW_AT + LAST))
        quantise(grouped_third, HALF, LAST)
        quantise(grouped_last, LAST, S)
        for m in range(LEAD_TILES):
            scatter(m, leads[m], 0, LEAD)

        rests = []
        for m in range(N_TILES):
            lo = LEAD if m < LEAD_TILES else 0
            rest = keep.tile([P, S - lo], F32, name=f"rest{m}", tag=f"rest{m}")
            if m == 0:
                for part_lo, part_hi in ((LEAD, LAST), (LAST, S)):
                    part_acc = psum.tile([P, S], F32, name=f"part_acc{part_lo}", tag="acc")
                    product(part_acc, m, part_lo, part_hi)
                    add_bias(rest[:, part_lo - lo : part_hi - lo], part_acc, m, part_lo, part_hi)
            else:
                acc = psum.tile([P, S], F32, name=f"acc{m}", tag="acc")
                if m < LEAD_TILES:
                    product(acc, m, LEAD, LAST)
                    product(acc, m, LAST, S)
                else:
                    product(acc, m, 0, S)
                add_bias(rest[:], acc, m, lo, S)
            rests.append(rest)

        for m in range(N_TILES):
            scatter(m, rests[m], LEAD if m < LEAD_TILES else 0, S)
            if m == N_TILES - 1:
                nc.scalar.dma_start(out=out[m * P : (m + 1) * P, :], in_=windows[m % WINDOWS][:], max_dma_last_dim=1024)
            else:
                nc.sync.dma_start(out=out[m * P : (m + 1) * P, :], in_=windows[m % WINDOWS][:])
